import numpy as np
import ml_dtypes


def mxq(x, axis, fmt="e4m3"):
    dtype, down = {"e4m3": (ml_dtypes.float8_e4m3fn, 7), "e5m2": (ml_dtypes.float8_e5m2, 14)}[fmt]
    v = np.moveaxis(np.asarray(x, np.float32).astype(ml_dtypes.bfloat16).astype(np.float64), axis, -1)
    blocks = v.reshape(v.shape[:-1] + (-1, 32))
    amax = np.abs(blocks).max(-1, keepdims=True)
    byte = np.maximum(np.where(amax > 0, np.frexp(amax)[1] - 1 + 127, 0) - down, 1)
    scale = np.exp2(byte - 127.0)
    codes = (blocks / scale).astype(np.float32).astype(dtype).astype(np.float64)
    return np.moveaxis((codes * scale).reshape(v.shape), -1, axis)


WIDE = False


def mx_kscale(k):
    if not WIDE:
        return np.ones(k)
    levels = np.array([10, -10, 5, -5, 0])
    if k % 512:
        return np.exp2(np.random.permutation(np.resize(levels, k // 32))).repeat(32)
    a = np.empty((k // 512, 16))
    for p in range(k // 512):
        a[p, :8] = np.random.permutation(np.resize(levels, 8))
        for g in range(8):
            far = levels[np.abs(levels - a[p, g]) >= 10]
            a[p, g + 8] = far[np.random.randint(len(far))]
    return np.exp2(a.ravel()).repeat(32)


def f64(x):
    return np.asarray(x).astype(np.float64)


def striped(idx):
    return np.tile(idx.reshape(-1, 16).T, (8, 1)).astype(np.uint16)


def unstriped(offs):
    return offs[:16].T.reshape(-1).astype(np.int64)


def striped8(idx):
    return np.concatenate([x.reshape(-1, 16).T for x in idx]).astype(np.uint16)


def runs(offs, k):
    lists = np.stack([offs[16 * r : 16 * r + 16].T.reshape(-1) for r in range(8)]).astype(np.int64)
    return lists[np.arange(k) % 512 // 64]


def pack_weight(w):
    k, n = w.shape
    w = f64(np.asarray(w, np.float32).astype(ml_dtypes.bfloat16)).reshape(k // 32, 32, n)
    amax = np.abs(w).max(1)
    byte = np.clip(np.where(amax > 0, np.frexp(amax)[1] - 1 + 127 - 7, 1), 1, 254)
    scaled = (w * np.exp2(127.0 - byte)[:, None, :]).reshape(k, n).astype(np.float32)
    words = np.ascontiguousarray(scaled.reshape(k // 512, 128, 4, n).transpose(0, 1, 3, 2)).astype(ml_dtypes.float8_e4m3fn).view(np.uint8)
    return words, np.ascontiguousarray(byte.astype(np.uint8).reshape(k // 512, 16, n))


def unpack_weight(words, scales):
    g, p, n, _ = words.shape
    vals = np.ascontiguousarray(words).view(ml_dtypes.float8_e4m3fn).astype(np.float64) * np.repeat(np.exp2(scales.astype(np.float64) - 127.0), 8, axis=1)[..., None]
    return vals.transpose(0, 1, 3, 2).reshape(g * 512, n)

def planes(y):
    n, m = y.shape
    v = y.astype(np.float32).astype(ml_dtypes.bfloat16).astype(np.float64).reshape(n // 32, 32, m)
    top = np.abs(v).max(1)
    byte = np.clip(np.where(top > 0, np.frexp(top)[1] - 1 + 127 - 7, 1), 1, 254)
    codes = (v * np.exp2(127.0 - byte)[:, None, :]).reshape(n, m).astype(np.float32).astype(ml_dtypes.float8_e4m3fn).view(np.uint8)
    words = codes.reshape(n // 512, 128, 4, m).transpose(0, 1, 3, 2)
    return np.ascontiguousarray(words), np.ascontiguousarray(byte.astype(np.uint8).reshape(n // 512, 16, m))


K, T, S, N, U = 512, 2048, 512, 512, 1024


def setup_inputs():
    n = np.random.standard_normal
    s = mx_kscale(K)[:, None]
    packed_xT = pack_weight(n((K, T)) * s)
    return {
        "x_words": packed_xT[0],
        "x_scales": packed_xT[1],
        "w1": (n((K, N)) / np.sqrt(K) / s).astype(np.float32),
        "par": n((N, U)).astype(np.float32),
        "vel": n((N, U)).astype(np.float32),
        "offs": striped(np.random.permutation(T)[:S]),
        "ent": striped8(np.stack([np.random.permutation(U)[:S] for _ in range(8)])),
    }


def reference(x_words, x_scales, w1, par, vel, offs, ent):
    xq = unpack_weight(x_words, x_scales)[:, unstriped(offs)]
    y = mxq(f64(w1), 0, "e4m3").T @ xq
    a = 0.75 * (f64(vel)[np.arange(N)[:, None], runs(ent, N)]) - (0.25 * y)
    o = f64(par)[np.arange(N)[:, None], runs(ent, N)] + 0.75 * a - (0.25 * y)
    out = f64(par).copy()
    out[np.arange(N)[:, None], runs(ent, N)] = o
    return (out,) + planes(out)

@@ -1,0 +1,165 @@
+from contextlib import ExitStack
+
+import concourse.mybir as mybir
+
+K, T, S, N, U = 512, 2048, 512, 512, 1024
+FLOPS = 2 * K * N * S
+
+F32 = mybir.dt.float32
+BF16 = mybir.dt.bfloat16
+I32 = mybir.dt.int32
+U32 = mybir.dt.uint32
+U16 = mybir.dt.uint16
+U8 = mybir.dt.uint8
+FP8X4 = mybir.dt.float8_e4m3fn_x4
+MULT = mybir.AluOpType.mult
+ADD = mybir.AluOpType.add
+COPY = mybir.ActivationFunctionType.Copy
+
+P = 128
+PACK = 4
+QUADRANT = 32
+CHUNK = 256
+CHUNKS = U // CHUNK
+VECTOR_CHUNKS = 2
+
+
+def tile_picked_snag_none_po_kernel(
+    tc, x_words, x_scales, w1, par, vel, offs, ent, out_0, out_1, out_2
+):
+    nc = tc.nc
+    par_rows = par.rearrange("(p t) c -> p t c", t=PACK)
+    vel_rows = vel.rearrange("(p t) c -> p t c", t=PACK)
+    out_rows = out_0.rearrange("(p t) c -> p t c", t=PACK)
+
+    with ExitStack() as ctx:
+        keep = ctx.enter_context(tc.tile_pool(name="keep", bufs=1))
+        psum = ctx.enter_context(tc.psum_pool(name="psum", bufs=1))
+
+        offs_sb = keep.tile([P, S // 16], U16, name="offs_sb")
+        ent_sb = keep.tile([P, S // 16], U16, name="ent_sb")
+        x_all = keep.tile([P, T], U32, name="x_all")
+        xs_all = keep.tile([P, T], U8, name="xs_all")
+        w_raw = keep.tile([P, PACK, N], F32, name="w_raw")
+        par_sb = [keep.tile([P, U], F32, name="par%d" % t) for t in range(PACK)]
+        vel_first = keep.tile([P, U], F32, name="vel_first")
+        vel_mid = keep.tile([P, 2 * U], F32, name="vel_mid")
+        vel_last = keep.tile([P, U], F32, name="vel_last")
+        vel_sb = [vel_first[:], vel_mid[:, :U], vel_mid[:, U:], vel_last[:]]
+
+        nc.vector.memset(xs_all[:].bitcast(I32), 0)
+        nc.sync.dma_start(offs_sb[:], offs)
+        nc.sync.dma_start(w_raw[:], w1.rearrange("(p j) c -> p j c", j=PACK))
+        for q in range(P // QUADRANT):
+            nc.scalar.dma_start(
+                xs_all[QUADRANT * q : QUADRANT * q + 4, :].bitcast(I32),
+                x_scales[0, 4 * q : 4 * q + 4, :].bitcast(I32),
+            )
+        nc.sync.dma_start(vel_first[:], vel_rows[:, 0, :])
+        nc.sync.dma_start(ent_sb[:], ent)
+        nc.sync.dma_start(x_all[:].bitcast(I32), x_words[0].rearrange("p c r -> p (c r)").bitcast(I32))
+        for t in range(3):
+            nc.sync.dma_start(par_sb[t][:], par_rows[:, t, :])
+        nc.sync.dma_start(vel_mid[:], vel.rearrange("(p t) c -> p (t c)", t=PACK)[:, U : 3 * U])
+        nc.sync.dma_start(vel_last[:], vel_rows[:, 3, :])
+        nc.sync.dma_start(par_sb[3][:], par_rows[:, 3, :])
+
+        x_codes = keep.tile([P, S], U32, name="x_codes", align_bytes=64)
+        x_bytes = keep.tile([P, S], U8, name="x_bytes", align_bytes=64)
+        nc.vector.tensor_copy(x_bytes[:], xs_all[:].indirect(offs_sb[:]))
+
+        w_codes = keep.tile([P, N], U32, name="w_codes", align_bytes=64)
+        w_bytes = keep.tile([P, N], U8, name="w_bytes", align_bytes=64)
+        w_view = w_raw[:].rearrange("p j (m t) -> p m t j", t=PACK)
+        w_dealt = []
+        for h in range(2):
+            dealt = keep.tile([P, N * 2], BF16, name="w_dealt%d" % h, align_bytes=64)
+            copy = nc.vector.tensor_copy if h == 0 else nc.scalar.copy
+            copy(dealt[:].rearrange("p (t m j) -> p m t j", t=2, j=PACK), w_view[:, :, 2 * h : 2 * h + 2, :])
+            w_dealt.append(dealt)
+
+        vel_picked = keep.tile([P, S], F32, name="vel_picked")
+        nc.vector.tensor_scalar(vel_picked[:], vel_first[:].indirect(ent_sb[:]), 0.5625, 0.0, MULT, ADD)
+        for h in range(2):
+            cols = slice(2 * P * h, 2 * P * (h + 1))
+            nc.vector.quantize_mx(w_codes[:, cols].bitcast(FP8X4), w_bytes[:, cols], w_dealt[h][:])
+        nc.vector.tensor_copy(x_codes[:], x_all[:].indirect(offs_sb[:]))
+
+        grad = []
+        for t in range(PACK):
+            acc = psum.tile([P, S], F32, name="acc%d" % t)
+            cols = slice(P * t, P * (t + 1))
+            nc.tensor.matmul_mx(
+                acc[:],
+                lhsT=w_codes[:, cols].bitcast(FP8X4),
+                lhsT_scale=w_bytes[:, cols],
+                rhs=x_codes[:].bitcast(FP8X4),
+                rhs_scale=x_bytes[:],
+                start=True,
+                stop=True,
+            )
+            scaled = keep.tile([P, S], F32, name="grad%d" % t)
+            nc.scalar.activation(scaled[:], acc[:], COPY, scale=-0.4375)
+            grad.append(scaled)
+
+        rounded = [
+            keep.tile([P, CHUNK, PACK], BF16, name="rounded%d" % c, align_bytes=64) for c in range(CHUNKS)
+        ]
+        mixed = {t: keep.tile([P, U], F32, name="mixed%d" % t) for t in range(1, PACK)}
+        picked = [keep.tile([P, S], F32, name="picked%d" % t) for t in range(PACK)]
+
+        def mix(t):
+            nc.vector.scalar_tensor_tensor(mixed[t][:], vel_sb[t], 0.5625, par_sb[t][:], MULT, ADD)
+
+        def pick(t):
+            nc.vector.tensor_copy(picked[t][:], mixed[t][:].indirect(ent_sb[:]))
+
+        def put(t):
+            nc.vector.tensor_tensor(par_sb[t][:].indirect(ent_sb[:]), picked[t][:], grad[t][:], ADD)
+            nc.sync.dma_start(out_rows[:, t, :], par_sb[t][:])
+            if t < PACK - 1:
+                for c in range(CHUNKS):
+                    src = par_sb[t][:, CHUNK * c : CHUNK * (c + 1)]
+                    if t == PACK - 2 and c < VECTOR_CHUNKS:
+                        nc.scalar.copy(rounded[c][:, :, t:], src.unsqueeze(2).to_broadcast([P, CHUNK, 2]))
+                    else:
+                        nc.scalar.copy(rounded[c][:, :, t], src)
+
+        nc.vector.tensor_tensor(picked[0][:], par_sb[0][:].indirect(ent_sb[:]), vel_picked[:], ADD)
+        put(0)
+        mix(1)
+        mix(2)
+        pick(1)
+        pick(2)
+        mix(3)
+        put(1)
+        pick(3)
+        put(2)
+        put(3)
+
+        last = PACK - 1
+        for c in range(CHUNKS):
+            src = par_sb[last][:, CHUNK * c : CHUNK * (c + 1)]
+            if c < VECTOR_CHUNKS:
+                nc.vector.tensor_copy(rounded[c][:, :, last], src)
+            else:
+                nc.scalar.copy(rounded[c][:, :, last], src)
+
+        out_codes = keep.tile([P, U], U32, name="out_codes", align_bytes=64)
+        out_bytes = keep.tile([P, U], U8, name="out_bytes", align_bytes=64)
+        words_out = out_1[0].rearrange("p c r -> p (c r)").bitcast(I32)
+        for c in range(CHUNKS):
+            cols = slice(CHUNK * c, CHUNK * (c + 1))
+            nc.vector.quantize_mx(
+                out_codes[:, cols].bitcast(FP8X4),
+                out_bytes[:, cols],
+                rounded[c][:].rearrange("p c t -> p (c t)"),
+            )
+            if c % 2 == 1:
+                pair = slice(CHUNK * (c - 1), CHUNK * (c + 1))
+                nc.sync.dma_start(words_out[:, pair], out_codes[:, pair].bitcast(I32))
+        for q in range(P // QUADRANT):
+            nc.sync.dma_start(
+                out_2[0, 4 * q : 4 * q + 4, :].bitcast(I32),
+                out_bytes[QUADRANT * q : QUADRANT * q + 4, :].bitcast(I32),
+            )

@@ -22,6 +22,7 @@ QUADRANT = 32
 CHUNK = 256
 CHUNKS = U // CHUNK
 VECTOR_CHUNKS = 2
+HALVES = (slice(0, U // 2), slice(U // 2, U))
 
 
 def tile_picked_snag_none_po_kernel(
@@ -34,6 +35,7 @@ def tile_picked_snag_none_po_kernel(
 
     with ExitStack() as ctx:
         keep = ctx.enter_context(tc.tile_pool(name="keep", bufs=1))
+        shared = ctx.enter_context(tc.tile_pool(name="shared", bufs=1))
         psum = ctx.enter_context(tc.psum_pool(name="psum", bufs=1))
 
         offs_sb = keep.tile([P, S // 16], U16, name="offs_sb")
@@ -42,30 +44,31 @@ def tile_picked_snag_none_po_kernel(
         xs_all = keep.tile([P, T], U8, name="xs_all")
         w_raw = keep.tile([P, PACK, N], F32, name="w_raw")
         par_sb = [keep.tile([P, U], F32, name="par%d" % t) for t in range(PACK)]
-        vel_first = keep.tile([P, U], F32, name="vel_first")
-        vel_mid = keep.tile([P, 2 * U], F32, name="vel_mid")
-        vel_last = keep.tile([P, U], F32, name="vel_last")
-        vel_sb = [vel_first[:], vel_mid[:, :U], vel_mid[:, U:], vel_last[:]]
+        vel_sb = [keep.tile([P, U], F32, name="vel%d" % t) for t in range(2)]
+        vel_late = shared.tile([P, 2 * U], F32, name="vel_late", offset=0, align_bytes=64)
 
         nc.vector.memset(xs_all[:].bitcast(I32), 0)
         nc.sync.dma_start(offs_sb[:], offs)
-        nc.sync.dma_start(w_raw[:], w1.rearrange("(p j) c -> p j c", j=PACK))
+        nc.sync.dma_start(x_all[:].bitcast(I32), x_words[0].rearrange("p c r -> p (c r)").bitcast(I32))
         for q in range(P // QUADRANT):
-            nc.scalar.dma_start(
+            nc.sync.dma_start(
                 xs_all[QUADRANT * q : QUADRANT * q + 4, :].bitcast(I32),
                 x_scales[0, 4 * q : 4 * q + 4, :].bitcast(I32),
             )
-        nc.sync.dma_start(vel_first[:], vel_rows[:, 0, :])
+        nc.sync.dma_start(w_raw[:], w1.rearrange("(p j) c -> p j c", j=PACK))
+        nc.sync.dma_start(vel_sb[0][:], vel_rows[:, 0, :])
+        for half in HALVES:
+            nc.sync.dma_start(par_sb[0][:, half], par_rows[:, 0, half])
         nc.sync.dma_start(ent_sb[:], ent)
-        nc.sync.dma_start(x_all[:].bitcast(I32), x_words[0].rearrange("p c r -> p (c r)").bitcast(I32))
-        for t in range(3):
-            nc.sync.dma_start(par_sb[t][:], par_rows[:, t, :])
-        nc.sync.dma_start(vel_mid[:], vel.rearrange("(p t) c -> p (t c)", t=PACK)[:, U : 3 * U])
-        nc.sync.dma_start(vel_last[:], vel_rows[:, 3, :])
+        nc.sync.dma_start(vel_sb[1][:], vel_rows[:, 1, :])
+        nc.sync.dma_start(par_sb[1][:], par_rows[:, 1, :])
+        nc.sync.dma_start(vel_late[:], vel.rearrange("(p t) c -> p (t c)", t=PACK)[:, 2 * U :])
+        nc.sync.dma_start(par_sb[2][:], par_rows[:, 2, :])
         nc.sync.dma_start(par_sb[3][:], par_rows[:, 3, :])
 
         x_codes = keep.tile([P, S], U32, name="x_codes", align_bytes=64)
         x_bytes = keep.tile([P, S], U8, name="x_bytes", align_bytes=64)
+        nc.vector.tensor_copy(x_codes[:], x_all[:].indirect(offs_sb[:]))
         nc.vector.tensor_copy(x_bytes[:], xs_all[:].indirect(offs_sb[:]))
 
         w_codes = keep.tile([P, N], U32, name="w_codes", align_bytes=64)
@@ -78,12 +81,9 @@ def tile_picked_snag_none_po_kernel(
             copy(dealt[:].rearrange("p (t m j) -> p m t j", t=2, j=PACK), w_view[:, :, 2 * h : 2 * h + 2, :])
             w_dealt.append(dealt)
 
-        vel_picked = keep.tile([P, S], F32, name="vel_picked")
-        nc.vector.tensor_scalar(vel_picked[:], vel_first[:].indirect(ent_sb[:]), 0.5625, 0.0, MULT, ADD)
         for h in range(2):
             cols = slice(2 * P * h, 2 * P * (h + 1))
             nc.vector.quantize_mx(w_codes[:, cols].bitcast(FP8X4), w_bytes[:, cols], w_dealt[h][:])
-        nc.vector.tensor_copy(x_codes[:], x_all[:].indirect(offs_sb[:]))
 
         grad = []
         for t in range(PACK):
@@ -101,21 +101,27 @@ def tile_picked_snag_none_po_kernel(
             scaled = keep.tile([P, S], F32, name="grad%d" % t)
             nc.scalar.activation(scaled[:], acc[:], COPY, scale=-0.4375)
             grad.append(scaled)
+            if t == 0:
+                vel_scaled = keep.tile([P, 3 * U], F32, name="vel_scaled")
+                nc.scalar.activation(vel_scaled[:, :U], vel_sb[1][:], COPY, scale=0.5625)
+        nc.scalar.activation(vel_scaled[:, U:], vel_late[:], COPY, scale=0.5625)
 
         rounded = [
-            keep.tile([P, CHUNK, PACK], BF16, name="rounded%d" % c, align_bytes=64) for c in range(CHUNKS)
+            shared.tile([P, CHUNK, PACK], BF16, name="rounded%d" % c, align_bytes=64, offset=2 * CHUNK * PACK * c)
+            for c in range(CHUNKS)
         ]
-        mixed = {t: keep.tile([P, U], F32, name="mixed%d" % t) for t in range(1, PACK)}
-        picked = [keep.tile([P, S], F32, name="picked%d" % t) for t in range(PACK)]
-
-        def mix(t):
-            nc.vector.scalar_tensor_tensor(mixed[t][:], vel_sb[t], 0.5625, par_sb[t][:], MULT, ADD)
-
-        def pick(t):
-            nc.vector.tensor_copy(picked[t][:], mixed[t][:].indirect(ent_sb[:]))
-
-        def put(t):
-            nc.vector.tensor_tensor(par_sb[t][:].indirect(ent_sb[:]), picked[t][:], grad[t][:], ADD)
+        for t in range(PACK):
+            mixed = keep.tile([P, U], F32, name="mixed")
+            moved = keep.tile([P, S], F32, name="moved%d" % t)
+            if t == 0:
+                for half in HALVES:
+                    nc.vector.scalar_tensor_tensor(
+                        mixed[:, half], vel_sb[0][:, half], 0.5625, par_sb[0][:, half], MULT, ADD
+                    )
+            else:
+                nc.gpsimd.tensor_tensor(mixed[:], vel_scaled[:, U * (t - 1) : U * t], par_sb[t][:], ADD)
+            nc.vector.tensor_tensor(moved[:], mixed[:].indirect(ent_sb[:]), grad[t][:], ADD)
+            nc.vector.tensor_copy(par_sb[t][:].indirect(ent_sb[:]), moved[:])
             nc.sync.dma_start(out_rows[:, t, :], par_sb[t][:])
             if t < PACK - 1:
                 for c in range(CHUNKS):
@@ -124,18 +130,6 @@ def tile_picked_snag_none_po_kernel(
                         nc.scalar.copy(rounded[c][:, :, t:], src.unsqueeze(2).to_broadcast([P, CHUNK, 2]))
                     else:
                         nc.scalar.copy(rounded[c][:, :, t], src)
-
-        nc.vector.tensor_tensor(picked[0][:], par_sb[0][:].indirect(ent_sb[:]), vel_picked[:], ADD)
-        put(0)
-        mix(1)
-        mix(2)
-        pick(1)
-        pick(2)
-        mix(3)
-        put(1)
-        pick(3)
-        put(2)
-        put(3)
 
         last = PACK - 1
         for c in range(CHUNKS):
@@ -155,11 +149,12 @@ def tile_picked_snag_none_po_kernel(
                 out_bytes[:, cols],
                 rounded[c][:].rearrange("p c t -> p (c t)"),
             )
-            if c % 2 == 1:
-                pair = slice(CHUNK * (c - 1), CHUNK * (c + 1))
-                nc.sync.dma_start(words_out[:, pair], out_codes[:, pair].bitcast(I32))
+            if c >= VECTOR_CHUNKS - 1:
+                ready = slice(0 if c < VECTOR_CHUNKS else CHUNK * c, CHUNK * (c + 1))
+                nc.sync.dma_start(words_out[:, ready], out_codes[:, ready].bitcast(I32))
         for q in range(P // QUADRANT):
-            nc.sync.dma_start(
+            queue = nc.sync if q % 2 else nc.scalar
+            queue.dma_start(
                 out_2[0, 4 * q : 4 * q + 4, :].bitcast(I32),
                 out_bytes[QUADRANT * q : QUADRANT * q + 4, :].bitcast(I32),
             )

@@ -44,17 +44,18 @@ def tile_picked_snag_none_po_kernel(
         xs_all = keep.tile([P, T], U8, name="xs_all")
         w_raw = keep.tile([P, PACK, N], F32, name="w_raw")
         par_sb = [keep.tile([P, U], F32, name="par%d" % t) for t in range(PACK)]
-        vel_sb = [keep.tile([P, U], F32, name="vel%d" % t) for t in range(2)]
+        vel_sb = [
+            keep.tile([P, U], F32, name="vel0"),
+            shared.tile([P, U], F32, name="vel1", offset=8 * U, align_bytes=64),
+        ]
         vel_late = shared.tile([P, 2 * U], F32, name="vel_late", offset=0, align_bytes=64)
 
         nc.vector.memset(xs_all[:].bitcast(I32), 0)
         nc.sync.dma_start(offs_sb[:], offs)
         nc.sync.dma_start(x_all[:].bitcast(I32), x_words[0].rearrange("p c r -> p (c r)").bitcast(I32))
-        for q in range(P // QUADRANT):
-            nc.sync.dma_start(
-                xs_all[QUADRANT * q : QUADRANT * q + 4, :].bitcast(I32),
-                x_scales[0, 4 * q : 4 * q + 4, :].bitcast(I32),
-            )
+        scale_rows = x_scales[0].bitcast(I32).rearrange("(q r) c -> r q c", r=4)
+        for r in range(4):
+            nc.sync.dma_start(xs_all[r:P:QUADRANT, :].bitcast(I32), scale_rows[r])
         nc.sync.dma_start(w_raw[:], w1.rearrange("(p j) c -> p j c", j=PACK))
         nc.sync.dma_start(vel_sb[0][:], vel_rows[:, 0, :])
         for half in HALVES:
@@ -87,24 +88,32 @@ def tile_picked_snag_none_po_kernel(
 
         grad = []
         for t in range(PACK):
-            acc = psum.tile([P, S], F32, name="acc%d" % t)
             cols = slice(P * t, P * (t + 1))
-            nc.tensor.matmul_mx(
-                acc[:],
-                lhsT=w_codes[:, cols].bitcast(FP8X4),
-                lhsT_scale=w_bytes[:, cols],
-                rhs=x_codes[:].bitcast(FP8X4),
-                rhs_scale=x_bytes[:],
-                start=True,
-                stop=True,
-            )
-            scaled = keep.tile([P, S], F32, name="grad%d" % t)
-            nc.scalar.activation(scaled[:], acc[:], COPY, scale=-0.4375)
+            if t < 2:
+                scaled = keep.tile([P, S], F32, name="grad%d" % t)
+            else:
+                scaled = shared.tile([P, S], F32, name="grad%d" % t, offset=8 * U + 4 * S * (t - 2), align_bytes=64)
+            for h in range(2):
+                entries = slice(S // 2 * h, S // 2 * (h + 1))
+                acc = psum.tile([P, S // 2], F32, name="acc%d_%d" % (t, h))
+                nc.tensor.matmul_mx(
+                    acc[:],
+                    lhsT=w_codes[:, cols].bitcast(FP8X4),
+                    lhsT_scale=w_bytes[:, cols],
+                    rhs=x_codes[:, entries].bitcast(FP8X4),
+                    rhs_scale=x_bytes[:, entries],
+                    start=True,
+                    stop=True,
+                )
+                nc.scalar.activation(scaled[:, entries], acc[:], COPY, scale=-0.4375)
             grad.append(scaled)
             if t == 0:
                 vel_scaled = keep.tile([P, 3 * U], F32, name="vel_scaled")
                 nc.scalar.activation(vel_scaled[:, :U], vel_sb[1][:], COPY, scale=0.5625)
-        nc.scalar.activation(vel_scaled[:, U:], vel_late[:], COPY, scale=0.5625)
+        for t in range(2):
+            nc.scalar.activation(
+                vel_scaled[:, U * (t + 1) : U * (t + 2)], vel_late[:, U * t : U * (t + 1)], COPY, scale=0.5625
+            )
 
         rounded = [
             shared.tile([P, CHUNK, PACK], BF16, name="rounded%d" % c, align_bytes=64, offset=2 * CHUNK * PACK * c)
@@ -152,9 +161,7 @@ def tile_picked_snag_none_po_kernel(
             if c >= VECTOR_CHUNKS - 1:
                 ready = slice(0 if c < VECTOR_CHUNKS else CHUNK * c, CHUNK * (c + 1))
                 nc.sync.dma_start(words_out[:, ready], out_codes[:, ready].bitcast(I32))
-        for q in range(P // QUADRANT):
-            queue = nc.sync if q % 2 else nc.scalar
-            queue.dma_start(
-                out_2[0, 4 * q : 4 * q + 4, :].bitcast(I32),
-                out_bytes[QUADRANT * q : QUADRANT * q + 4, :].bitcast(I32),
-            )
+        scale_rows_out = out_2[0].bitcast(I32).rearrange("(q r) c -> r q c", r=4)
+        for r in range(4):
+            queue = nc.sync if r % 2 else nc.scalar
+            queue.dma_start(scale_rows_out[r], out_bytes[r:P:QUADRANT, :].bitcast(I32))

@@ -22,7 +22,11 @@ QUADRANT = 32
 CHUNK = 256
 CHUNKS = U // CHUNK
 VECTOR_CHUNKS = 2
-HALVES = (slice(0, U // 2), slice(U // 2, U))
+ORDER = (0, 3, 2, 1)
+VEL_FACTOR = 0.5625
+GRAD_FACTOR = -0.4375
+COLUMN_HALVES = (slice(0, U // 2), slice(U // 2, U))
+ENTRY_HALVES = (slice(0, S // 2), slice(S // 2, S))
 
 
 def tile_picked_snag_none_po_kernel(
@@ -32,6 +36,7 @@ def tile_picked_snag_none_po_kernel(
     par_rows = par.rearrange("(p t) c -> p t c", t=PACK)
     vel_rows = vel.rearrange("(p t) c -> p t c", t=PACK)
     out_rows = out_0.rearrange("(p t) c -> p t c", t=PACK)
+    first, second, third, last = ORDER
 
     with ExitStack() as ctx:
         keep = ctx.enter_context(tc.tile_pool(name="keep", bufs=1))
@@ -40,37 +45,46 @@ def tile_picked_snag_none_po_kernel(
 
         offs_sb = keep.tile([P, S // 16], U16, name="offs_sb")
         ent_sb = keep.tile([P, S // 16], U16, name="ent_sb")
-        x_all = keep.tile([P, T], U32, name="x_all")
-        xs_all = keep.tile([P, T], U8, name="xs_all")
-        w_raw = keep.tile([P, PACK, N], F32, name="w_raw")
-        par_sb = [keep.tile([P, U], F32, name="par%d" % t) for t in range(PACK)]
-        vel_sb = [
-            keep.tile([P, U], F32, name="vel0"),
-            shared.tile([P, U], F32, name="vel1", offset=8 * U, align_bytes=64),
-        ]
-        vel_late = shared.tile([P, 2 * U], F32, name="vel_late", offset=0, align_bytes=64)
+        def placed(shape, dtype, name, offset):
+            return shared.tile(shape, dtype, name=name, offset=offset, align_bytes=64)
 
-        nc.vector.memset(xs_all[:].bitcast(I32), 0)
-        nc.sync.dma_start(offs_sb[:], offs)
-        nc.sync.dma_start(x_all[:].bitcast(I32), x_words[0].rearrange("p c r -> p (c r)").bitcast(I32))
-        scale_rows = x_scales[0].bitcast(I32).rearrange("(q r) c -> r q c", r=4)
-        for r in range(4):
-            nc.sync.dma_start(xs_all[r:P:QUADRANT, :].bitcast(I32), scale_rows[r])
-        nc.sync.dma_start(w_raw[:], w1.rearrange("(p j) c -> p j c", j=PACK))
-        nc.sync.dma_start(vel_sb[0][:], vel_rows[:, 0, :])
-        for half in HALVES:
-            nc.sync.dma_start(par_sb[0][:, half], par_rows[:, 0, half])
-        nc.sync.dma_start(ent_sb[:], ent)
-        nc.sync.dma_start(vel_sb[1][:], vel_rows[:, 1, :])
-        nc.sync.dma_start(par_sb[1][:], par_rows[:, 1, :])
-        nc.sync.dma_start(vel_late[:], vel.rearrange("(p t) c -> p (t c)", t=PACK)[:, 2 * U :])
-        nc.sync.dma_start(par_sb[2][:], par_rows[:, 2, :])
-        nc.sync.dma_start(par_sb[3][:], par_rows[:, 3, :])
-
+        row = 4 * U
+        lap = 64
+        w_raw = placed([P, PACK, N], F32, "w_raw", 5 * row)
+        vel_late = placed([P, 2 * U], F32, "vel_late", lap)
+        x_all = placed([P, T], U32, "x_all", 2 * row)
+        xs_all = placed([P, T], U8, "xs_all", 8 * row)
+        par_at = {third: 5 * row // 2, second: 7 * row // 2, last: 5 * row, first: 10 * row}
+        par_sb = [placed([P, U], F32, "par%d" % t, par_at[t]) for t in range(PACK)]
+        vel_first = placed([P, U], F32, "vel_first", 7 * row + lap)
+        vel_second_at = 8 * row + T - lap
+        vel_second = placed([P, U], F32, "vel_second", vel_second_at)
         x_codes = keep.tile([P, S], U32, name="x_codes", align_bytes=64)
         x_bytes = keep.tile([P, S], U8, name="x_bytes", align_bytes=64)
+        spread_bytes = keep.tile([P, S], U8, name="spread_bytes", align_bytes=64)
+
+        nc.vector.memset(xs_all[:].bitcast(I32), 0)
+        nc.gpsimd.memset(x_bytes[:].bitcast(I32), 0)
+        x_rows = x_words[0].rearrange("p c r -> p (c r)").bitcast(I32)
+        nc.sync.dma_start(x_all[:, : T // 2].bitcast(I32), x_rows[:, : T // 2])
+        nc.sync.dma_start(offs_sb[:], offs)
+        nc.sync.dma_start(xs_all[0:P:8, :].bitcast(I32), x_scales[0].bitcast(I32))
+        nc.sync.dma_start(x_all[:, T // 2 :].bitcast(I32), x_rows[:, T // 2 :])
+        nc.sync.dma_start(ent_sb[:], ent)
+        nc.sync.dma_start(w_raw[:], w1.rearrange("(p j) c -> p j c", j=PACK))
+        nc.sync.dma_start(par_sb[first][:], par_rows[:, first, :])
+
+        nc.vector.tensor_copy(spread_bytes[:], xs_all[:].indirect(offs_sb[:]))
+        for r in range(4):
+            nc.sync.dma_start(x_bytes[r:P:QUADRANT, :].bitcast(I32), spread_bytes[8 * r : P : QUADRANT, :].bitcast(I32))
+        for half in COLUMN_HALVES:
+            nc.sync.dma_start(vel_first[:, half], vel_rows[:, first, half])
+        nc.sync.dma_start(vel_second[:], vel_rows[:, second, :])
+
         nc.vector.tensor_copy(x_codes[:], x_all[:].indirect(offs_sb[:]))
-        nc.vector.tensor_copy(x_bytes[:], xs_all[:].indirect(offs_sb[:]))
+        nc.sync.dma_start(par_sb[second][:], par_rows[:, second, :])
+        nc.sync.dma_start(vel_late[:], vel.rearrange("(p t) c -> p (t c)", t=PACK)[:, U * last : U * (third + 1)])
+        nc.sync.dma_start(par_sb[third][:], par_rows[:, third, :])
 
         w_codes = keep.tile([P, N], U32, name="w_codes", align_bytes=64)
         w_bytes = keep.tile([P, N], U8, name="w_bytes", align_bytes=64)
@@ -81,20 +95,16 @@ def tile_picked_snag_none_po_kernel(
             copy = nc.vector.tensor_copy if h == 0 else nc.scalar.copy
             copy(dealt[:].rearrange("p (t m j) -> p m t j", t=2, j=PACK), w_view[:, :, 2 * h : 2 * h + 2, :])
             w_dealt.append(dealt)
+        nc.sync.dma_start(par_sb[last][:], par_rows[:, last, :])
 
         for h in range(2):
             cols = slice(2 * P * h, 2 * P * (h + 1))
             nc.vector.quantize_mx(w_codes[:, cols].bitcast(FP8X4), w_bytes[:, cols], w_dealt[h][:])
 
-        grad = []
-        for t in range(PACK):
+        banks = {}
+        for t in ORDER:
             cols = slice(P * t, P * (t + 1))
-            if t < 2:
-                scaled = keep.tile([P, S], F32, name="grad%d" % t)
-            else:
-                scaled = shared.tile([P, S], F32, name="grad%d" % t, offset=8 * U + 4 * S * (t - 2), align_bytes=64)
-            for h in range(2):
-                entries = slice(S // 2 * h, S // 2 * (h + 1))
+            for h, entries in enumerate(ENTRY_HALVES):
                 acc = psum.tile([P, S // 2], F32, name="acc%d_%d" % (t, h))
                 nc.tensor.matmul_mx(
                     acc[:],
@@ -105,48 +115,50 @@ def tile_picked_snag_none_po_kernel(
                     start=True,
                     stop=True,
                 )
-                nc.scalar.activation(scaled[:, entries], acc[:], COPY, scale=-0.4375)
-            grad.append(scaled)
-            if t == 0:
-                vel_scaled = keep.tile([P, 3 * U], F32, name="vel_scaled")
-                nc.scalar.activation(vel_scaled[:, :U], vel_sb[1][:], COPY, scale=0.5625)
-        for t in range(2):
+                banks[t, h] = acc
+
+        def leave_banks(t, scaled):
+            for h, entries in enumerate(ENTRY_HALVES):
+                nc.scalar.activation(scaled[:, entries], banks[t, h][:], COPY, scale=GRAD_FACTOR)
+            return scaled
+
+        grad = {first: leave_banks(first, keep.tile([P, S], F32, name="grad%d" % first))}
+        vel_scaled = {t: keep.tile([P, U], F32, name="vel_scaled%d" % t) for t in ORDER[1:]}
+        nc.scalar.activation(vel_scaled[second][:], vel_second[:], COPY, scale=VEL_FACTOR)
+        for i, t in enumerate((second, third)):
+            grad[t] = leave_banks(
+                t, shared.tile([P, S], F32, name="grad%d" % t, offset=vel_second_at + 4 * S * i, align_bytes=64)
+            )
+        for t in (third, last):
             nc.scalar.activation(
-                vel_scaled[:, U * (t + 1) : U * (t + 2)], vel_late[:, U * t : U * (t + 1)], COPY, scale=0.5625
+                vel_scaled[t][:], vel_late[:, U * (t - last) : U * (t - last + 1)], COPY, scale=VEL_FACTOR
             )
 
         rounded = [
             shared.tile([P, CHUNK, PACK], BF16, name="rounded%d" % c, align_bytes=64, offset=2 * CHUNK * PACK * c)
             for c in range(CHUNKS)
         ]
-        for t in range(PACK):
-            mixed = keep.tile([P, U], F32, name="mixed")
+        for t in ORDER:
             moved = keep.tile([P, S], F32, name="moved%d" % t)
-            if t == 0:
-                for half in HALVES:
+            mixed = keep.tile([P, U], F32, name="mixed")
+            if t == first:
+                for half in COLUMN_HALVES:
                     nc.vector.scalar_tensor_tensor(
-                        mixed[:, half], vel_sb[0][:, half], 0.5625, par_sb[0][:, half], MULT, ADD
+                        mixed[:, half], vel_first[:, half], VEL_FACTOR, par_sb[first][:, half], MULT, ADD
                     )
             else:
-                nc.gpsimd.tensor_tensor(mixed[:], vel_scaled[:, U * (t - 1) : U * t], par_sb[t][:], ADD)
+                nc.gpsimd.tensor_tensor(mixed[:], vel_scaled[t][:], par_sb[t][:], ADD)
             nc.vector.tensor_tensor(moved[:], mixed[:].indirect(ent_sb[:]), grad[t][:], ADD)
             nc.vector.tensor_copy(par_sb[t][:].indirect(ent_sb[:]), moved[:])
             nc.sync.dma_start(out_rows[:, t, :], par_sb[t][:])
-            if t < PACK - 1:
-                for c in range(CHUNKS):
-                    src = par_sb[t][:, CHUNK * c : CHUNK * (c + 1)]
-                    if t == PACK - 2 and c < VECTOR_CHUNKS:
-                        nc.scalar.copy(rounded[c][:, :, t:], src.unsqueeze(2).to_broadcast([P, CHUNK, 2]))
-                    else:
-                        nc.scalar.copy(rounded[c][:, :, t], src)
-
-        last = PACK - 1
-        for c in range(CHUNKS):
-            src = par_sb[last][:, CHUNK * c : CHUNK * (c + 1)]
-            if c < VECTOR_CHUNKS:
-                nc.vector.tensor_copy(rounded[c][:, :, last], src)
-            else:
-                nc.scalar.copy(rounded[c][:, :, last], src)
+            for c in range(CHUNKS):
+                src = par_sb[t][:, CHUNK * c : CHUNK * (c + 1)]
+                copy = nc.vector.tensor_copy if t == last and c < VECTOR_CHUNKS else nc.scalar.copy
+                copy(rounded[c][:, :, t], src)
+            if t == first:
+                grad[last] = leave_banks(
+                    last, shared.tile([P, S], F32, name="grad%d" % last, offset=2 * row, align_bytes=64)
+                )
 
         out_codes = keep.tile([P, U], U32, name="out_codes", align_bytes=64)
         out_bytes = keep.tile([P, U], U8, name="out_bytes", align_bytes=64)

@@ -25,7 +25,7 @@ VECTOR_CHUNKS = 2
 ORDER = (0, 3, 2, 1)
 VEL_FACTOR = 0.5625
 GRAD_FACTOR = -0.4375
-COLUMN_HALVES = (slice(0, U // 2), slice(U // 2, U))
+PIECES = (slice(0, 5 * U // 8), slice(5 * U // 8, U))
 ENTRY_HALVES = (slice(0, S // 2), slice(S // 2, S))
 
 
@@ -54,10 +54,13 @@ def tile_picked_snag_none_po_kernel(
         vel_late = placed([P, 2 * U], F32, "vel_late", lap)
         x_all = placed([P, T], U32, "x_all", 2 * row)
         xs_all = placed([P, T], U8, "xs_all", 8 * row)
-        par_at = {third: 5 * row // 2, second: 7 * row // 2, last: 5 * row, first: 10 * row}
+        par_at = {second: 5 * row // 2, third: 5 * row, last: 6 * row, first: 7 * row + lap}
         par_sb = [placed([P, U], F32, "par%d" % t, par_at[t]) for t in range(PACK)]
-        vel_first = placed([P, U], F32, "vel_first", 7 * row + lap)
-        vel_second_at = 8 * row + T - lap
+        vel_first = [
+            keep.tile([P, PIECES[0].stop], F32, name="vel_first0"),
+            placed([P, U - PIECES[0].stop], F32, "vel_first1", 8 * row + T - lap),
+        ]
+        vel_second_at = 7 * row // 2
         vel_second = placed([P, U], F32, "vel_second", vel_second_at)
         x_codes = keep.tile([P, S], U32, name="x_codes", align_bytes=64)
         x_bytes = keep.tile([P, S], U8, name="x_bytes", align_bytes=64)
@@ -72,19 +75,19 @@ def tile_picked_snag_none_po_kernel(
         nc.sync.dma_start(x_all[:, T // 2 :].bitcast(I32), x_rows[:, T // 2 :])
         nc.sync.dma_start(ent_sb[:], ent)
         nc.sync.dma_start(w_raw[:], w1.rearrange("(p j) c -> p j c", j=PACK))
-        nc.sync.dma_start(par_sb[first][:], par_rows[:, first, :])
+        nc.sync.dma_start(vel_first[0][:], vel_rows[:, first, PIECES[0]])
 
         nc.vector.tensor_copy(spread_bytes[:], xs_all[:].indirect(offs_sb[:]))
         for r in range(4):
             nc.sync.dma_start(x_bytes[r:P:QUADRANT, :].bitcast(I32), spread_bytes[8 * r : P : QUADRANT, :].bitcast(I32))
-        for half in COLUMN_HALVES:
-            nc.sync.dma_start(vel_first[:, half], vel_rows[:, first, half])
-        nc.sync.dma_start(vel_second[:], vel_rows[:, second, :])
+        nc.sync.dma_start(par_sb[first][:, PIECES[0]], par_rows[:, first, PIECES[0]])
+        nc.sync.dma_start(vel_first[1][:], vel_rows[:, first, PIECES[1]])
+        nc.sync.dma_start(par_sb[first][:, PIECES[1]], par_rows[:, first, PIECES[1]])
 
         nc.vector.tensor_copy(x_codes[:], x_all[:].indirect(offs_sb[:]))
+        nc.sync.dma_start(vel_second[:], vel_rows[:, second, :])
         nc.sync.dma_start(par_sb[second][:], par_rows[:, second, :])
         nc.sync.dma_start(vel_late[:], vel.rearrange("(p t) c -> p (t c)", t=PACK)[:, U * last : U * (third + 1)])
-        nc.sync.dma_start(par_sb[third][:], par_rows[:, third, :])
 
         w_codes = keep.tile([P, N], U32, name="w_codes", align_bytes=64)
         w_bytes = keep.tile([P, N], U8, name="w_bytes", align_bytes=64)
@@ -95,6 +98,7 @@ def tile_picked_snag_none_po_kernel(
             copy = nc.vector.tensor_copy if h == 0 else nc.scalar.copy
             copy(dealt[:].rearrange("p (t m j) -> p m t j", t=2, j=PACK), w_view[:, :, 2 * h : 2 * h + 2, :])
             w_dealt.append(dealt)
+        nc.sync.dma_start(par_sb[third][:], par_rows[:, third, :])
         nc.sync.dma_start(par_sb[last][:], par_rows[:, last, :])
 
         for h in range(2):
@@ -142,9 +146,9 @@ def tile_picked_snag_none_po_kernel(
             moved = keep.tile([P, S], F32, name="moved%d" % t)
             mixed = keep.tile([P, U], F32, name="mixed")
             if t == first:
-                for half in COLUMN_HALVES:
+                for h, half in enumerate(PIECES):
                     nc.vector.scalar_tensor_tensor(
-                        mixed[:, half], vel_first[:, half], VEL_FACTOR, par_sb[first][:, half], MULT, ADD
+                        mixed[:, half], vel_first[h][:], VEL_FACTOR, par_sb[first][:, half], MULT, ADD
                     )
             else:
                 nc.gpsimd.tensor_tensor(mixed[:], vel_scaled[t][:], par_sb[t][:], ADD)

@@ -22,10 +22,11 @@ QUADRANT = 32
 CHUNK = 256
 CHUNKS = U // CHUNK
 VECTOR_CHUNKS = 2
+ROW_PAIRS = (slice(0, 2), slice(2, 4))
 ORDER = (0, 3, 2, 1)
 VEL_FACTOR = 0.5625
 GRAD_FACTOR = -0.4375
-PIECES = (slice(0, 5 * U // 8), slice(5 * U // 8, U))
+PIECES = (slice(0, U // 2), slice(U // 2, U))
 ENTRY_HALVES = (slice(0, S // 2), slice(S // 2, S))
 
 
@@ -56,10 +57,7 @@ def tile_picked_snag_none_po_kernel(
         xs_all = placed([P, T], U8, "xs_all", 8 * row)
         par_at = {second: 5 * row // 2, third: 5 * row, last: 6 * row, first: 7 * row + lap}
         par_sb = [placed([P, U], F32, "par%d" % t, par_at[t]) for t in range(PACK)]
-        vel_first = [
-            keep.tile([P, PIECES[0].stop], F32, name="vel_first0"),
-            placed([P, U - PIECES[0].stop], F32, "vel_first1", 8 * row + T - lap),
-        ]
+        vel_first = keep.tile([P, U], F32, name="vel_first")
         vel_second_at = 7 * row // 2
         vel_second = placed([P, U], F32, "vel_second", vel_second_at)
         x_codes = keep.tile([P, S], U32, name="x_codes", align_bytes=64)
@@ -68,21 +66,20 @@ def tile_picked_snag_none_po_kernel(
 
         nc.vector.memset(xs_all[:].bitcast(I32), 0)
         nc.gpsimd.memset(x_bytes[:].bitcast(I32), 0)
-        x_rows = x_words[0].rearrange("p c r -> p (c r)").bitcast(I32)
-        nc.sync.dma_start(x_all[:, : T // 2].bitcast(I32), x_rows[:, : T // 2])
+        w_rows = w1.rearrange("(p j) c -> p j c", j=PACK)
+        nc.sync.dma_start(w_raw[:, ROW_PAIRS[0], :], w_rows[:, ROW_PAIRS[0], :])
         nc.sync.dma_start(offs_sb[:], offs)
         nc.sync.dma_start(xs_all[0:P:8, :].bitcast(I32), x_scales[0].bitcast(I32))
-        nc.sync.dma_start(x_all[:, T // 2 :].bitcast(I32), x_rows[:, T // 2 :])
+        nc.sync.dma_start(x_all[:].bitcast(I32), x_words[0].rearrange("p c r -> p (c r)").bitcast(I32))
         nc.sync.dma_start(ent_sb[:], ent)
-        nc.sync.dma_start(w_raw[:], w1.rearrange("(p j) c -> p j c", j=PACK))
-        nc.sync.dma_start(vel_first[0][:], vel_rows[:, first, PIECES[0]])
+        nc.sync.dma_start(w_raw[:, ROW_PAIRS[1], :], w_rows[:, ROW_PAIRS[1], :])
+        nc.sync.dma_start(vel_first[:], vel_rows[:, first, :])
 
         nc.vector.tensor_copy(spread_bytes[:], xs_all[:].indirect(offs_sb[:]))
         for r in range(4):
             nc.sync.dma_start(x_bytes[r:P:QUADRANT, :].bitcast(I32), spread_bytes[8 * r : P : QUADRANT, :].bitcast(I32))
-        nc.sync.dma_start(par_sb[first][:, PIECES[0]], par_rows[:, first, PIECES[0]])
-        nc.sync.dma_start(vel_first[1][:], vel_rows[:, first, PIECES[1]])
-        nc.sync.dma_start(par_sb[first][:, PIECES[1]], par_rows[:, first, PIECES[1]])
+        for half in PIECES:
+            nc.sync.dma_start(par_sb[first][:, half], par_rows[:, first, half])
 
         nc.vector.tensor_copy(x_codes[:], x_all[:].indirect(offs_sb[:]))
         nc.sync.dma_start(vel_second[:], vel_rows[:, second, :])
@@ -91,12 +88,13 @@ def tile_picked_snag_none_po_kernel(
 
         w_codes = keep.tile([P, N], U32, name="w_codes", align_bytes=64)
         w_bytes = keep.tile([P, N], U8, name="w_bytes", align_bytes=64)
-        w_view = w_raw[:].rearrange("p j (m t) -> p m t j", t=PACK)
+        w_view = w_raw[:].rearrange("p j (a m t) -> p a t m j", m=2, t=PACK)
         w_dealt = []
-        for h in range(2):
+        for h, copy in enumerate((nc.vector.tensor_copy, nc.scalar.copy)):
             dealt = keep.tile([P, N * 2], BF16, name="w_dealt%d" % h, align_bytes=64)
-            copy = nc.vector.tensor_copy if h == 0 else nc.scalar.copy
-            copy(dealt[:].rearrange("p (t m j) -> p m t j", t=2, j=PACK), w_view[:, :, 2 * h : 2 * h + 2, :])
+            dealt_view = dealt[:].rearrange("p (t a m j) -> p a t m j", t=2, m=2, j=PACK)
+            for pair_copy, pair in zip((nc.scalar.copy, copy), ROW_PAIRS):
+                pair_copy(dealt_view[:, :, :, :, pair], w_view[:, :, 2 * h : 2 * h + 2, :, pair])
             w_dealt.append(dealt)
         nc.sync.dma_start(par_sb[third][:], par_rows[:, third, :])
         nc.sync.dma_start(par_sb[last][:], par_rows[:, last, :])
@@ -146,9 +144,9 @@ def tile_picked_snag_none_po_kernel(
             moved = keep.tile([P, S], F32, name="moved%d" % t)
             mixed = keep.tile([P, U], F32, name="mixed")
             if t == first:
-                for h, half in enumerate(PIECES):
+                for half in PIECES:
                     nc.vector.scalar_tensor_tensor(
-                        mixed[:, half], vel_first[h][:], VEL_FACTOR, par_sb[first][:, half], MULT, ADD
+                        mixed[:, half], vel_first[:, half], VEL_FACTOR, par_sb[first][:, half], MULT, ADD
                     )
             else:
                 nc.gpsimd.tensor_tensor(mixed[:], vel_scaled[t][:], par_sb[t][:], ADD)

@@ -51,9 +51,9 @@ def tile_picked_snag_none_po_kernel(
 
         row = 4 * U
         lap = 64
-        w_raw = placed([P, PACK, N], F32, "w_raw", 5 * row)
+        w_raw = placed([P, PACK, N], F32, "w_raw", 2 * row)
         vel_late = placed([P, 2 * U], F32, "vel_late", lap)
-        x_all = placed([P, T], U32, "x_all", 2 * row)
+        x_all = placed([P, T], U32, "x_all", 5 * row)
         xs_all = placed([P, T], U8, "xs_all", 8 * row)
         par_at = {second: 5 * row // 2, third: 5 * row, last: 6 * row, first: 7 * row + lap}
         par_sb = [placed([P, U], F32, "par%d" % t, par_at[t]) for t in range(PACK)]
@@ -70,9 +70,9 @@ def tile_picked_snag_none_po_kernel(
         nc.sync.dma_start(w_raw[:, ROW_PAIRS[0], :], w_rows[:, ROW_PAIRS[0], :])
         nc.sync.dma_start(offs_sb[:], offs)
         nc.sync.dma_start(xs_all[0:P:8, :].bitcast(I32), x_scales[0].bitcast(I32))
-        nc.sync.dma_start(x_all[:].bitcast(I32), x_words[0].rearrange("p c r -> p (c r)").bitcast(I32))
-        nc.sync.dma_start(ent_sb[:], ent)
         nc.sync.dma_start(w_raw[:, ROW_PAIRS[1], :], w_rows[:, ROW_PAIRS[1], :])
+        nc.sync.dma_start(ent_sb[:], ent)
+        nc.sync.dma_start(x_all[:].bitcast(I32), x_words[0].rearrange("p c r -> p (c r)").bitcast(I32))
         nc.sync.dma_start(vel_first[:], vel_rows[:, first, :])
 
         nc.vector.tensor_copy(spread_bytes[:], xs_all[:].indirect(offs_sb[:]))
@@ -81,10 +81,6 @@ def tile_picked_snag_none_po_kernel(
         for half in PIECES:
             nc.sync.dma_start(par_sb[first][:, half], par_rows[:, first, half])
 
-        nc.vector.tensor_copy(x_codes[:], x_all[:].indirect(offs_sb[:]))
-        nc.sync.dma_start(vel_second[:], vel_rows[:, second, :])
-        nc.sync.dma_start(par_sb[second][:], par_rows[:, second, :])
-        nc.sync.dma_start(vel_late[:], vel.rearrange("(p t) c -> p (t c)", t=PACK)[:, U * last : U * (third + 1)])
 
         w_codes = keep.tile([P, N], U32, name="w_codes", align_bytes=64)
         w_bytes = keep.tile([P, N], U8, name="w_bytes", align_bytes=64)
@@ -96,18 +92,25 @@ def tile_picked_snag_none_po_kernel(
             for pair_copy, pair in zip((nc.scalar.copy, copy), ROW_PAIRS):
                 pair_copy(dealt_view[:, :, :, :, pair], w_view[:, :, 2 * h : 2 * h + 2, :, pair])
             w_dealt.append(dealt)
-        nc.sync.dma_start(par_sb[third][:], par_rows[:, third, :])
-        nc.sync.dma_start(par_sb[last][:], par_rows[:, last, :])
+        nc.sync.dma_start(vel_second[:], vel_rows[:, second, :])
+        nc.sync.dma_start(par_sb[second][:], par_rows[:, second, :])
+        nc.sync.dma_start(vel_late[:], vel.rearrange("(p t) c -> p (t c)", t=PACK)[:, U * last : U * (third + 1)])
 
         for h in range(2):
             cols = slice(2 * P * h, 2 * P * (h + 1))
             nc.vector.quantize_mx(w_codes[:, cols].bitcast(FP8X4), w_bytes[:, cols], w_dealt[h][:])
 
+        for h, entries in enumerate(ENTRY_HALVES):
+            nc.vector.tensor_copy(x_codes[:, entries], x_all[:].indirect(offs_sb[:, 16 * h : 16 * (h + 1)]))
+        nc.sync.dma_start(par_sb[third][:], par_rows[:, third, :])
+        nc.sync.dma_start(par_sb[last][:], par_rows[:, last, :])
+
         banks = {}
         for t in ORDER:
             cols = slice(P * t, P * (t + 1))
-            for h, entries in enumerate(ENTRY_HALVES):
-                acc = psum.tile([P, S // 2], F32, name="acc%d_%d" % (t, h))
+            banks[t] = []
+            for entries in ENTRY_HALVES if t == first else (slice(0, S),):
+                acc = psum.tile([P, entries.stop - entries.start], F32, name="acc%d_%d" % (t, entries.start))
                 nc.tensor.matmul_mx(
                     acc[:],
                     lhsT=w_codes[:, cols].bitcast(FP8X4),
@@ -117,11 +120,11 @@ def tile_picked_snag_none_po_kernel(
                     start=True,
                     stop=True,
                 )
-                banks[t, h] = acc
+                banks[t].append((entries, acc))
 
         def leave_banks(t, scaled):
-            for h, entries in enumerate(ENTRY_HALVES):
-                nc.scalar.activation(scaled[:, entries], banks[t, h][:], COPY, scale=GRAD_FACTOR)
+            for entries, acc in banks[t]:
+                nc.scalar.activation(scaled[:, entries], acc[:], COPY, scale=GRAD_FACTOR)
             return scaled
 
         grad = {first: leave_banks(first, keep.tile([P, S], F32, name="grad%d" % first))}

@@ -159,7 +159,15 @@ def tile_picked_snag_none_po_kernel(
             for c in range(CHUNKS):
                 src = par_sb[t][:, CHUNK * c : CHUNK * (c + 1)]
                 copy = nc.vector.tensor_copy if t == last and c < VECTOR_CHUNKS else nc.scalar.copy
-                copy(rounded[c][:, :, t], src)
+                if t == last and c == CHUNKS - 1:
+                    for part in (slice(0, CHUNK // 2), slice(CHUNK // 2, CHUNK)):
+                        copy(rounded[c][:, part, t], src[:, part])
+                elif t == last and c == VECTOR_CHUNKS - 1:
+                    cut = CHUNK - CHUNK // 4
+                    nc.vector.tensor_copy(rounded[c][:, 0:cut, t], src[:, 0:cut])
+                    nc.scalar.copy(rounded[c][:, cut:CHUNK, t], src[:, cut:CHUNK])
+                else:
+                    copy(rounded[c][:, :, t], src)
             if t == first:
                 grad[last] = leave_banks(
                     last, shared.tile([P, S], F32, name="grad%d" % last, offset=2 * row, align_bytes=64)
@@ -168,15 +176,17 @@ def tile_picked_snag_none_po_kernel(
         out_codes = keep.tile([P, U], U32, name="out_codes", align_bytes=64)
         out_bytes = keep.tile([P, U], U8, name="out_bytes", align_bytes=64)
         words_out = out_1[0].rearrange("p c r -> p (c r)").bitcast(I32)
-        for c in range(CHUNKS):
-            cols = slice(CHUNK * c, CHUNK * (c + 1))
+        edges = (0, CHUNK, 2 * CHUNK, 3 * CHUNK, U - CHUNK // 2, U)
+        store_from = {2 * CHUNK: 0, U - CHUNK // 2: 2 * CHUNK, U: U - CHUNK // 2}
+        for start, stop in zip(edges, edges[1:]):
+            c, at = divmod(start, CHUNK)
             nc.vector.quantize_mx(
-                out_codes[:, cols].bitcast(FP8X4),
-                out_bytes[:, cols],
-                rounded[c][:].rearrange("p c t -> p (c t)"),
+                out_codes[:, start:stop].bitcast(FP8X4),
+                out_bytes[:, start:stop],
+                rounded[c][:, at : at + stop - start, :].rearrange("p c t -> p (c t)"),
             )
-            if c >= VECTOR_CHUNKS - 1:
-                ready = slice(0 if c < VECTOR_CHUNKS else CHUNK * c, CHUNK * (c + 1))
+            if stop in store_from:
+                ready = slice(store_from[stop], stop)
                 nc.sync.dma_start(words_out[:, ready], out_codes[:, ready].bitcast(I32))
         scale_rows_out = out_2[0].bitcast(I32).rearrange("(q r) c -> r q c", r=4)
         for r in range(4):

@@ -19,14 +19,18 @@ COPY = mybir.ActivationFunctionType.Copy
 P = 128
 PACK = 4
 QUADRANT = 32
+SCALE_ROWS = 4
+BLOCK_PARTITIONS = 8
+GROUP = 16
 CHUNK = 256
 CHUNKS = U // CHUNK
-VECTOR_CHUNKS = 2
+VECTOR_COLUMNS = 2 * CHUNK - CHUNK // 4
+LAST_PIECE = CHUNK // 2
 ROW_PAIRS = (slice(0, 2), slice(2, 4))
 ORDER = (0, 3, 2, 1)
 VEL_FACTOR = 0.5625
 GRAD_FACTOR = -0.4375
-PIECES = (slice(0, U // 2), slice(U // 2, U))
+COLUMN_HALVES = (slice(0, U // 2), slice(U // 2, U))
 ENTRY_HALVES = (slice(0, S // 2), slice(S // 2, S))
 
 
@@ -44,8 +48,9 @@ def tile_picked_snag_none_po_kernel(
         shared = ctx.enter_context(tc.tile_pool(name="shared", bufs=1))
         psum = ctx.enter_context(tc.psum_pool(name="psum", bufs=1))
 
-        offs_sb = keep.tile([P, S // 16], U16, name="offs_sb")
-        ent_sb = keep.tile([P, S // 16], U16, name="ent_sb")
+        offs_sb = keep.tile([P, S // GROUP], U16, name="offs_sb")
+        ent_sb = keep.tile([P, S // GROUP], U16, name="ent_sb")
+
         def placed(shape, dtype, name, offset):
             return shared.tile(shape, dtype, name=name, offset=offset, align_bytes=64)
 
@@ -66,30 +71,33 @@ def tile_picked_snag_none_po_kernel(
 
         nc.vector.memset(xs_all[:].bitcast(I32), 0)
         nc.gpsimd.memset(x_bytes[:].bitcast(I32), 0)
+
         w_rows = w1.rearrange("(p j) c -> p j c", j=PACK)
         nc.sync.dma_start(w_raw[:, ROW_PAIRS[0], :], w_rows[:, ROW_PAIRS[0], :])
         nc.sync.dma_start(offs_sb[:], offs)
-        nc.sync.dma_start(xs_all[0:P:8, :].bitcast(I32), x_scales[0].bitcast(I32))
+        nc.sync.dma_start(xs_all[0:P:BLOCK_PARTITIONS, :].bitcast(I32), x_scales[0].bitcast(I32))
         nc.sync.dma_start(w_raw[:, ROW_PAIRS[1], :], w_rows[:, ROW_PAIRS[1], :])
         nc.sync.dma_start(ent_sb[:], ent)
         nc.sync.dma_start(x_all[:].bitcast(I32), x_words[0].rearrange("p c r -> p (c r)").bitcast(I32))
         nc.sync.dma_start(vel_first[:], vel_rows[:, first, :])
 
         nc.vector.tensor_copy(spread_bytes[:], xs_all[:].indirect(offs_sb[:]))
-        for r in range(4):
-            nc.sync.dma_start(x_bytes[r:P:QUADRANT, :].bitcast(I32), spread_bytes[8 * r : P : QUADRANT, :].bitcast(I32))
-        for half in PIECES:
+        for r in range(SCALE_ROWS):
+            nc.sync.dma_start(
+                x_bytes[r:P:QUADRANT, :].bitcast(I32),
+                spread_bytes[BLOCK_PARTITIONS * r : P : QUADRANT, :].bitcast(I32),
+            )
+        for half in COLUMN_HALVES:
             nc.sync.dma_start(par_sb[first][:, half], par_rows[:, first, half])
-
 
         w_codes = keep.tile([P, N], U32, name="w_codes", align_bytes=64)
         w_bytes = keep.tile([P, N], U8, name="w_bytes", align_bytes=64)
         w_view = w_raw[:].rearrange("p j (a m t) -> p a t m j", m=2, t=PACK)
         w_dealt = []
-        for h, copy in enumerate((nc.vector.tensor_copy, nc.scalar.copy)):
+        for h, second_pair_copy in enumerate((nc.vector.tensor_copy, nc.scalar.copy)):
             dealt = keep.tile([P, N * 2], BF16, name="w_dealt%d" % h, align_bytes=64)
             dealt_view = dealt[:].rearrange("p (t a m j) -> p a t m j", t=2, m=2, j=PACK)
-            for pair_copy, pair in zip((nc.scalar.copy, copy), ROW_PAIRS):
+            for pair_copy, pair in zip((nc.scalar.copy, second_pair_copy), ROW_PAIRS):
                 pair_copy(dealt_view[:, :, :, :, pair], w_view[:, :, 2 * h : 2 * h + 2, :, pair])
             w_dealt.append(dealt)
         nc.sync.dma_start(vel_second[:], vel_rows[:, second, :])
@@ -100,8 +108,9 @@ def tile_picked_snag_none_po_kernel(
             cols = slice(2 * P * h, 2 * P * (h + 1))
             nc.vector.quantize_mx(w_codes[:, cols].bitcast(FP8X4), w_bytes[:, cols], w_dealt[h][:])
 
-        for h, entries in enumerate(ENTRY_HALVES):
-            nc.vector.tensor_copy(x_codes[:, entries], x_all[:].indirect(offs_sb[:, 16 * h : 16 * (h + 1)]))
+        for entries in ENTRY_HALVES:
+            listed = offs_sb[:, entries.start // GROUP : entries.stop // GROUP]
+            nc.vector.tensor_copy(x_codes[:, entries], x_all[:].indirect(listed))
         nc.sync.dma_start(par_sb[third][:], par_rows[:, third, :])
         nc.sync.dma_start(par_sb[last][:], par_rows[:, last, :])
 
@@ -131,23 +140,24 @@ def tile_picked_snag_none_po_kernel(
         vel_scaled = {t: keep.tile([P, U], F32, name="vel_scaled%d" % t) for t in ORDER[1:]}
         nc.scalar.activation(vel_scaled[second][:], vel_second[:], COPY, scale=VEL_FACTOR)
         for i, t in enumerate((second, third)):
-            grad[t] = leave_banks(
-                t, shared.tile([P, S], F32, name="grad%d" % t, offset=vel_second_at + 4 * S * i, align_bytes=64)
-            )
+            grad[t] = leave_banks(t, placed([P, S], F32, "grad%d" % t, vel_second_at + 4 * S * i))
         for t in (third, last):
             nc.scalar.activation(
                 vel_scaled[t][:], vel_late[:, U * (t - last) : U * (t - last + 1)], COPY, scale=VEL_FACTOR
             )
 
-        rounded = [
-            shared.tile([P, CHUNK, PACK], BF16, name="rounded%d" % c, align_bytes=64, offset=2 * CHUNK * PACK * c)
-            for c in range(CHUNKS)
-        ]
+        rounded = [placed([P, CHUNK, PACK], BF16, "rounded%d" % c, 2 * CHUNK * PACK * c) for c in range(CHUNKS)]
+
+        def round_columns(copy, t, start, stop):
+            c, at = divmod(start, CHUNK)
+            copy(rounded[c][:, at : at + stop - start, t], par_sb[t][:, start:stop])
+
+        chunk_edges = set(range(0, U + 1, CHUNK))
         for t in ORDER:
             moved = keep.tile([P, S], F32, name="moved%d" % t)
             mixed = keep.tile([P, U], F32, name="mixed")
             if t == first:
-                for half in PIECES:
+                for half in COLUMN_HALVES:
                     nc.vector.scalar_tensor_tensor(
                         mixed[:, half], vel_first[:, half], VEL_FACTOR, par_sb[first][:, half], MULT, ADD
                     )
@@ -156,39 +166,30 @@ def tile_picked_snag_none_po_kernel(
             nc.vector.tensor_tensor(moved[:], mixed[:].indirect(ent_sb[:]), grad[t][:], ADD)
             nc.vector.tensor_copy(par_sb[t][:].indirect(ent_sb[:]), moved[:])
             nc.sync.dma_start(out_rows[:, t, :], par_sb[t][:])
-            for c in range(CHUNKS):
-                src = par_sb[t][:, CHUNK * c : CHUNK * (c + 1)]
-                copy = nc.vector.tensor_copy if t == last and c < VECTOR_CHUNKS else nc.scalar.copy
-                if t == last and c == CHUNKS - 1:
-                    for part in (slice(0, CHUNK // 2), slice(CHUNK // 2, CHUNK)):
-                        copy(rounded[c][:, part, t], src[:, part])
-                elif t == last and c == VECTOR_CHUNKS - 1:
-                    cut = CHUNK - CHUNK // 4
-                    nc.vector.tensor_copy(rounded[c][:, 0:cut, t], src[:, 0:cut])
-                    nc.scalar.copy(rounded[c][:, cut:CHUNK, t], src[:, cut:CHUNK])
-                else:
-                    copy(rounded[c][:, :, t], src)
+            edges = sorted(chunk_edges | {VECTOR_COLUMNS, U - LAST_PIECE} if t == last else chunk_edges)
+            for start, stop in zip(edges, edges[1:]):
+                on_vector = t == last and stop <= VECTOR_COLUMNS
+                round_columns(nc.vector.tensor_copy if on_vector else nc.scalar.copy, t, start, stop)
             if t == first:
-                grad[last] = leave_banks(
-                    last, shared.tile([P, S], F32, name="grad%d" % last, offset=2 * row, align_bytes=64)
-                )
+                grad[last] = leave_banks(last, placed([P, S], F32, "grad%d" % last, 2 * row))
 
         out_codes = keep.tile([P, U], U32, name="out_codes", align_bytes=64)
-        out_bytes = keep.tile([P, U], U8, name="out_bytes", align_bytes=64)
+        out_bytes = keep.tile([P, U // 2], U8, name="out_bytes", align_bytes=64)
         words_out = out_1[0].rearrange("p c r -> p (c r)").bitcast(I32)
-        edges = (0, CHUNK, 2 * CHUNK, 3 * CHUNK, U - CHUNK // 2, U)
-        store_from = {2 * CHUNK: 0, U - CHUNK // 2: 2 * CHUNK, U: U - CHUNK // 2}
+        edges = sorted(chunk_edges | {U - LAST_PIECE})
+        store_from = {U // 2: 0, U - LAST_PIECE: U // 2, U: U - LAST_PIECE}
         for start, stop in zip(edges, edges[1:]):
             c, at = divmod(start, CHUNK)
+            side, side_at = divmod(start, U // 2)
             nc.vector.quantize_mx(
                 out_codes[:, start:stop].bitcast(FP8X4),
-                out_bytes[:, start:stop],
+                out_bytes[SCALE_ROWS * side : P, side_at : side_at + stop - start],
                 rounded[c][:, at : at + stop - start, :].rearrange("p c t -> p (c t)"),
             )
             if stop in store_from:
                 ready = slice(store_from[stop], stop)
                 nc.sync.dma_start(words_out[:, ready], out_codes[:, ready].bitcast(I32))
-        scale_rows_out = out_2[0].bitcast(I32).rearrange("(q r) c -> r q c", r=4)
-        for r in range(4):
-            queue = nc.sync if r % 2 else nc.scalar
-            queue.dma_start(scale_rows_out[r], out_bytes[r:P:QUADRANT, :].bitcast(I32))
+        scale_rows_out = out_2[0].bitcast(I32).rearrange("(q r) (side w) -> q side r w", r=SCALE_ROWS, side=2)
+        for q in range(P // QUADRANT):
+            queue = nc.sync if q % 2 else nc.scalar
+            queue.dma_start(scale_rows_out[q], out_bytes[QUADRANT * q : QUADRANT * q + 2 * SCALE_ROWS, :].bitcast(I32))

@@ -24,13 +24,13 @@ BLOCK_PARTITIONS = 8
 GROUP = 16
 CHUNK = 256
 CHUNKS = U // CHUNK
-VECTOR_COLUMNS = 2 * CHUNK - CHUNK // 4
+VECTOR_COLUMNS = CHUNK + CHUNK // 2
+GPSIMD_FROM = 2 * CHUNK + CHUNK // 2
 LAST_PIECE = CHUNK // 2
 ROW_PAIRS = (slice(0, 2), slice(2, 4))
 ORDER = (0, 3, 2, 1)
 VEL_FACTOR = 0.5625
 GRAD_FACTOR = -0.4375
-COLUMN_HALVES = (slice(0, U // 2), slice(U // 2, U))
 ENTRY_HALVES = (slice(0, S // 2), slice(S // 2, S))
 
 
@@ -56,15 +56,14 @@ def tile_picked_snag_none_po_kernel(
 
         row = 4 * U
         lap = 64
-        w_raw = placed([P, PACK, N], F32, "w_raw", 2 * row)
-        vel_late = placed([P, 2 * U], F32, "vel_late", lap)
-        x_all = placed([P, T], U32, "x_all", 5 * row)
-        xs_all = placed([P, T], U8, "xs_all", 8 * row)
-        par_at = {second: 5 * row // 2, third: 5 * row, last: 6 * row, first: 7 * row + lap}
-        par_sb = [placed([P, U], F32, "par%d" % t, par_at[t]) for t in range(PACK)]
-        vel_first = keep.tile([P, U], F32, name="vel_first")
-        vel_second_at = 7 * row // 2
-        vel_second = placed([P, U], F32, "vel_second", vel_second_at)
+        w_raw = placed([P, PACK, N], F32, "w_raw", row)
+        x_all = placed([P, T], U32, "x_all", 6 * row)
+        xs_all = placed([P, T], U8, "xs_all", 11 * row)
+        par_at = {second: lap, third: 2 * row + lap, last: 6 * row + lap}
+        vel_at = {first: 10 * row + lap, second: row + lap, third: 5 * row + lap, last: 8 * row - lap}
+        par_sb = {t: placed([P, U], F32, "par%d" % t, par_at[t]) for t in ORDER[1:]}
+        par_sb[first] = keep.tile([P, U], F32, name="par_first")
+        vel_sb = {t: placed([P, U], F32, "vel%d" % t, vel_at[t]) for t in ORDER}
         x_codes = keep.tile([P, S], U32, name="x_codes", align_bytes=64)
         x_bytes = keep.tile([P, S], U8, name="x_bytes", align_bytes=64)
         spread_bytes = keep.tile([P, S], U8, name="spread_bytes", align_bytes=64)
@@ -79,7 +78,7 @@ def tile_picked_snag_none_po_kernel(
         nc.sync.dma_start(w_raw[:, ROW_PAIRS[1], :], w_rows[:, ROW_PAIRS[1], :])
         nc.sync.dma_start(ent_sb[:], ent)
         nc.sync.dma_start(x_all[:].bitcast(I32), x_words[0].rearrange("p c r -> p (c r)").bitcast(I32))
-        nc.sync.dma_start(vel_first[:], vel_rows[:, first, :])
+        nc.sync.dma_start(par_sb[first][:], par_rows[:, first, :])
 
         nc.vector.tensor_copy(spread_bytes[:], xs_all[:].indirect(offs_sb[:]))
         for r in range(SCALE_ROWS):
@@ -87,8 +86,7 @@ def tile_picked_snag_none_po_kernel(
                 x_bytes[r:P:QUADRANT, :].bitcast(I32),
                 spread_bytes[BLOCK_PARTITIONS * r : P : QUADRANT, :].bitcast(I32),
             )
-        for half in COLUMN_HALVES:
-            nc.sync.dma_start(par_sb[first][:, half], par_rows[:, first, half])
+        nc.sync.dma_start(vel_sb[first][:], vel_rows[:, first, :])
 
         w_codes = keep.tile([P, N], U32, name="w_codes", align_bytes=64)
         w_bytes = keep.tile([P, N], U8, name="w_bytes", align_bytes=64)
@@ -100,9 +98,9 @@ def tile_picked_snag_none_po_kernel(
             for pair_copy, pair in zip((nc.scalar.copy, second_pair_copy), ROW_PAIRS):
                 pair_copy(dealt_view[:, :, :, :, pair], w_view[:, :, 2 * h : 2 * h + 2, :, pair])
             w_dealt.append(dealt)
-        nc.sync.dma_start(vel_second[:], vel_rows[:, second, :])
         nc.sync.dma_start(par_sb[second][:], par_rows[:, second, :])
-        nc.sync.dma_start(vel_late[:], vel.rearrange("(p t) c -> p (t c)", t=PACK)[:, U * last : U * (third + 1)])
+        nc.sync.dma_start(vel_sb[second][:], vel_rows[:, second, :])
+        nc.sync.dma_start(par_sb[third][:], par_rows[:, third, :])
 
         for h in range(2):
             cols = slice(2 * P * h, 2 * P * (h + 1))
@@ -111,8 +109,9 @@ def tile_picked_snag_none_po_kernel(
         for entries in ENTRY_HALVES:
             listed = offs_sb[:, entries.start // GROUP : entries.stop // GROUP]
             nc.vector.tensor_copy(x_codes[:, entries], x_all[:].indirect(listed))
-        nc.sync.dma_start(par_sb[third][:], par_rows[:, third, :])
+        nc.sync.dma_start(vel_sb[third][:], vel_rows[:, third, :])
         nc.sync.dma_start(par_sb[last][:], par_rows[:, last, :])
+        nc.sync.dma_start(vel_sb[last][:], vel_rows[:, last, :])
 
         banks = {}
         for t in ORDER:
@@ -131,47 +130,76 @@ def tile_picked_snag_none_po_kernel(
                 )
                 banks[t].append((entries, acc))
 
-        def leave_banks(t, scaled):
-            for entries, acc in banks[t]:
-                nc.scalar.activation(scaled[:, entries], acc[:], COPY, scale=GRAD_FACTOR)
-            return scaled
+        def listed_by_ent(table, entries):
+            return table[:].indirect(ent_sb[:, entries.start // GROUP : entries.stop // GROUP])
 
-        grad = {first: leave_banks(first, keep.tile([P, S], F32, name="grad%d" % first))}
-        vel_scaled = {t: keep.tile([P, U], F32, name="vel_scaled%d" % t) for t in ORDER[1:]}
-        nc.scalar.activation(vel_scaled[second][:], vel_second[:], COPY, scale=VEL_FACTOR)
-        for i, t in enumerate((second, third)):
-            grad[t] = leave_banks(t, placed([P, S], F32, "grad%d" % t, vel_second_at + 4 * S * i))
-        for t in (third, last):
-            nc.scalar.activation(
-                vel_scaled[t][:], vel_late[:, U * (t - last) : U * (t - last + 1)], COPY, scale=VEL_FACTOR
+        whole = slice(0, S)
+        par_got = {t: keep.tile([P, S], F32, name="par_got%d" % t) for t in ORDER}
+        vel_got = {t: keep.tile([P, S], F32, name="vel_got%d" % t) for t in ORDER[:-1]}
+        vel_got[last] = placed([P, S], F32, "vel_got_last", 12 * row)
+        partial = {t: keep.tile([P, S], F32, name="partial%d" % t) for t in ORDER}
+        moved = {t: keep.tile([P, S], F32, name="moved%d" % t) for t in ORDER}
+        grad = {
+            second: keep.tile([P, S], F32, name="grad_second"),
+            third: placed([P, S], F32, "grad_third", vel_at[second]),
+            last: placed([P, S], F32, "grad_last", vel_at[third]),
+        }
+
+        nc.scalar.activation(par_got[first][:], listed_by_ent(par_sb[first], whole), COPY)
+        for entries, acc in banks[first]:
+            nc.vector.scalar_tensor_tensor(
+                partial[first][:, entries], acc[:], GRAD_FACTOR, par_got[first][:, entries], MULT, ADD
             )
+        for entries, engine in zip(ENTRY_HALVES, (nc.vector, nc.gpsimd)):
+            nc.scalar.activation(
+                vel_got[first][:, entries], listed_by_ent(vel_sb[first], entries), COPY, scale=VEL_FACTOR
+            )
+            engine.tensor_tensor(moved[first][:, entries], partial[first][:, entries], vel_got[first][:, entries], ADD)
+        for entries in ENTRY_HALVES:
+            nc.vector.tensor_copy(listed_by_ent(par_sb[first], entries), moved[first][:, entries])
+        nc.vector.tensor_scalar_mul(grad[second][:], banks[second][0][1][:], GRAD_FACTOR)
+        for t in ORDER[1:]:
+            if t != second:
+                nc.scalar.activation(grad[t][:], banks[t][0][1][:], COPY, scale=GRAD_FACTOR)
+            nc.scalar.activation(par_got[t][:], listed_by_ent(par_sb[t], whole), COPY)
+            nc.scalar.activation(vel_got[t][:], listed_by_ent(vel_sb[t], whole), COPY, scale=VEL_FACTOR)
+            nc.gpsimd.tensor_tensor(partial[t][:], par_got[t][:], grad[t][:], ADD)
+            nc.gpsimd.tensor_tensor(moved[t][:], partial[t][:], vel_got[t][:], ADD)
+            nc.vector.tensor_copy(listed_by_ent(par_sb[t], whole), moved[t][:])
+        for t in ORDER:
+            nc.sync.dma_start(out_rows[:, t, :], par_sb[t][:])
 
-        rounded = [placed([P, CHUNK, PACK], BF16, "rounded%d" % c, 2 * CHUNK * PACK * c) for c in range(CHUNKS)]
+        chunk_bytes = 2 * CHUNK * PACK
+        staged = placed([P, PACK, VECTOR_COLUMNS], BF16, "staged", vel_at[last] + lap - 2 * PACK * VECTOR_COLUMNS)
+        rounded = [keep.tile([P, CHUNK, PACK], BF16, name="rounded0", align_bytes=64)]
+        rounded_at = [vel_at[last] + lap, vel_at[last] + lap + chunk_bytes, 12 * row]
+        rounded.extend(placed([P, CHUNK, PACK], BF16, "rounded%d" % (c + 1), at) for c, at in enumerate(rounded_at))
+
+        def gpsimd_round(out, in_):
+            nc.gpsimd.tensor_scalar(out, in_, 1.0, -0.0, MULT, ADD)
 
         def round_columns(copy, t, start, stop):
             c, at = divmod(start, CHUNK)
             copy(rounded[c][:, at : at + stop - start, t], par_sb[t][:, start:stop])
 
         chunk_edges = set(range(0, U + 1, CHUNK))
+        vector_edges = (0, CHUNK, VECTOR_COLUMNS)
         for t in ORDER:
-            moved = keep.tile([P, S], F32, name="moved%d" % t)
-            mixed = keep.tile([P, U], F32, name="mixed")
-            if t == first:
-                for half in COLUMN_HALVES:
-                    nc.vector.scalar_tensor_tensor(
-                        mixed[:, half], vel_first[:, half], VEL_FACTOR, par_sb[first][:, half], MULT, ADD
+            if t == last:
+                for start, stop in zip(vector_edges, vector_edges[1:]):
+                    nc.vector.tensor_copy(staged[:, t, start:stop], par_sb[t][:, start:stop])
+                for c, (start, stop) in enumerate(zip(vector_edges, vector_edges[1:])):
+                    nc.vector.tensor_copy(
+                        rounded[c][:, : stop - start, :].rearrange("p (a i) t -> p a t i", i=PACK),
+                        staged[:, :, start:stop].rearrange("p t (a i) -> p a t i", i=PACK),
                     )
             else:
-                nc.gpsimd.tensor_tensor(mixed[:], vel_scaled[t][:], par_sb[t][:], ADD)
-            nc.vector.tensor_tensor(moved[:], mixed[:].indirect(ent_sb[:]), grad[t][:], ADD)
-            nc.vector.tensor_copy(par_sb[t][:].indirect(ent_sb[:]), moved[:])
-            nc.sync.dma_start(out_rows[:, t, :], par_sb[t][:])
-            edges = sorted(chunk_edges | {VECTOR_COLUMNS, U - LAST_PIECE} if t == last else chunk_edges)
+                nc.scalar.copy(staged[:, t, :], par_sb[t][:, :VECTOR_COLUMNS])
+            more = {first: set(), last: {U - LAST_PIECE}}.get(t, {GPSIMD_FROM})
+            edges = sorted(e for e in chunk_edges | more | {VECTOR_COLUMNS} if e >= VECTOR_COLUMNS)
             for start, stop in zip(edges, edges[1:]):
-                on_vector = t == last and stop <= VECTOR_COLUMNS
-                round_columns(nc.vector.tensor_copy if on_vector else nc.scalar.copy, t, start, stop)
-            if t == first:
-                grad[last] = leave_banks(last, placed([P, S], F32, "grad%d" % last, 2 * row))
+                on_gpsimd = t in (second, third) and start >= GPSIMD_FROM
+                round_columns(gpsimd_round if on_gpsimd else nc.scalar.copy, t, start, stop)
 
         out_codes = keep.tile([P, U], U32, name="out_codes", align_bytes=64)
         out_bytes = keep.tile([P, U // 2], U8, name="out_bytes", align_bytes=64)

@@ -77,8 +77,8 @@ def tile_picked_snag_none_po_kernel(
         nc.sync.dma_start(xs_all[0:P:BLOCK_PARTITIONS, :].bitcast(I32), x_scales[0].bitcast(I32))
         nc.sync.dma_start(w_raw[:, ROW_PAIRS[1], :], w_rows[:, ROW_PAIRS[1], :])
         nc.sync.dma_start(ent_sb[:], ent)
-        nc.sync.dma_start(x_all[:].bitcast(I32), x_words[0].rearrange("p c r -> p (c r)").bitcast(I32))
         nc.sync.dma_start(par_sb[first][:], par_rows[:, first, :])
+        nc.sync.dma_start(x_all[:].bitcast(I32), x_words[0].rearrange("p c r -> p (c r)").bitcast(I32))
 
         nc.vector.tensor_copy(spread_bytes[:], xs_all[:].indirect(offs_sb[:]))
         for r in range(SCALE_ROWS):
@@ -140,7 +140,7 @@ def tile_picked_snag_none_po_kernel(
         partial = {t: keep.tile([P, S], F32, name="partial%d" % t) for t in ORDER}
         moved = {t: keep.tile([P, S], F32, name="moved%d" % t) for t in ORDER}
         grad = {
-            second: keep.tile([P, S], F32, name="grad_second"),
+            second: placed([P, S], F32, "grad_second", vel_at[first]),
             third: placed([P, S], F32, "grad_third", vel_at[second]),
             last: placed([P, S], F32, "grad_last", vel_at[third]),
         }
@@ -150,14 +150,13 @@ def tile_picked_snag_none_po_kernel(
             nc.vector.scalar_tensor_tensor(
                 partial[first][:, entries], acc[:], GRAD_FACTOR, par_got[first][:, entries], MULT, ADD
             )
-        for entries, engine in zip(ENTRY_HALVES, (nc.vector, nc.gpsimd)):
+        for entries in ENTRY_HALVES:
             nc.scalar.activation(
                 vel_got[first][:, entries], listed_by_ent(vel_sb[first], entries), COPY, scale=VEL_FACTOR
             )
-            engine.tensor_tensor(moved[first][:, entries], partial[first][:, entries], vel_got[first][:, entries], ADD)
-        for entries in ENTRY_HALVES:
-            nc.vector.tensor_copy(listed_by_ent(par_sb[first], entries), moved[first][:, entries])
+            nc.vector.tensor_tensor(moved[first][:, entries], partial[first][:, entries], vel_got[first][:, entries], ADD)
         nc.vector.tensor_scalar_mul(grad[second][:], banks[second][0][1][:], GRAD_FACTOR)
+        nc.vector.tensor_copy(listed_by_ent(par_sb[first], whole), moved[first][:])
         for t in ORDER[1:]:
             if t != second:
                 nc.scalar.activation(grad[t][:], banks[t][0][1][:], COPY, scale=GRAD_FACTOR)
@@ -169,55 +168,49 @@ def tile_picked_snag_none_po_kernel(
         for t in ORDER:
             nc.sync.dma_start(out_rows[:, t, :], par_sb[t][:])
 
-        chunk_bytes = 2 * CHUNK * PACK
-        staged = placed([P, PACK, VECTOR_COLUMNS], BF16, "staged", vel_at[last] + lap - 2 * PACK * VECTOR_COLUMNS)
-        rounded = [keep.tile([P, CHUNK, PACK], BF16, name="rounded0", align_bytes=64)]
-        rounded_at = [vel_at[last] + lap, vel_at[last] + lap + chunk_bytes, 12 * row]
-        rounded.extend(placed([P, CHUNK, PACK], BF16, "rounded%d" % (c + 1), at) for c, at in enumerate(rounded_at))
+        edges = (0, VECTOR_COLUMNS, GPSIMD_FROM, U)
+        low, middle, high = (slice(start, stop) for start, stop in zip(edges, edges[1:]))
+        staged = placed([P, PACK, VECTOR_COLUMNS], BF16, "staged", 12 * row)
+        rounded_low = keep.tile([P, VECTOR_COLUMNS, PACK], BF16, name="rounded_low", align_bytes=64)
+        middle_bytes = 2 * PACK * (middle.stop - middle.start)
+        rounded_middle = placed([P, middle.stop - middle.start, PACK], BF16, "rounded_middle", vel_at[last])
+        rounded_high = placed([P, high.stop - high.start, PACK], BF16, "rounded_high", vel_at[last] + middle_bytes)
 
         def gpsimd_round(out, in_):
             nc.gpsimd.tensor_scalar(out, in_, 1.0, -0.0, MULT, ADD)
 
-        def round_columns(copy, t, start, stop):
-            c, at = divmod(start, CHUNK)
-            copy(rounded[c][:, at : at + stop - start, t], par_sb[t][:, start:stop])
-
-        chunk_edges = set(range(0, U + 1, CHUNK))
-        vector_edges = (0, CHUNK, VECTOR_COLUMNS)
-        for t in ORDER:
-            if t == last:
-                for start, stop in zip(vector_edges, vector_edges[1:]):
-                    nc.vector.tensor_copy(staged[:, t, start:stop], par_sb[t][:, start:stop])
-                for c, (start, stop) in enumerate(zip(vector_edges, vector_edges[1:])):
-                    nc.vector.tensor_copy(
-                        rounded[c][:, : stop - start, :].rearrange("p (a i) t -> p a t i", i=PACK),
-                        staged[:, :, start:stop].rearrange("p t (a i) -> p a t i", i=PACK),
-                    )
-            else:
-                nc.scalar.copy(staged[:, t, :], par_sb[t][:, :VECTOR_COLUMNS])
-            more = {first: set(), last: {U - LAST_PIECE}}.get(t, {GPSIMD_FROM})
-            edges = sorted(e for e in chunk_edges | more | {VECTOR_COLUMNS} if e >= VECTOR_COLUMNS)
-            for start, stop in zip(edges, edges[1:]):
-                on_gpsimd = t in (second, third) and start >= GPSIMD_FROM
-                round_columns(gpsimd_round if on_gpsimd else nc.scalar.copy, t, start, stop)
+        nc.scalar.copy(rounded_middle[:, :, first], par_sb[first][:, middle])
+        nc.scalar.copy(rounded_high[:, :, first], par_sb[first][:, high])
+        gpsimd_round(staged[:, first, :], par_sb[first][:, low])
+        for t in (second, third):
+            nc.scalar.copy(rounded_middle[:, :, t], par_sb[t][:, middle])
+            nc.scalar.copy(staged[:, t, :], par_sb[t][:, low])
+            gpsimd_round(rounded_high[:, :, t], par_sb[t][:, high])
+        pieces = [(middle, rounded_middle[:])]
+        for at, stop in ((0, CHUNK), (CHUNK, CHUNK + LAST_PIECE)):
+            pieces.append((slice(high.start + at, high.start + stop), rounded_high[:, at:stop, :]))
+        for columns, piece in pieces:
+            nc.scalar.copy(piece[:, :, last], par_sb[last][:, columns])
+        low_halves = (slice(0, VECTOR_COLUMNS // 2), slice(VECTOR_COLUMNS // 2, VECTOR_COLUMNS))
+        for half in low_halves:
+            nc.vector.tensor_copy(staged[:, last, half], par_sb[last][:, half])
+        for half in low_halves:
+            nc.vector.tensor_copy(
+                rounded_low[:, half, :].rearrange("p (a i) t -> p a t i", i=PACK),
+                staged[:, :, half].rearrange("p t (a i) -> p a t i", i=PACK),
+            )
+        pieces.insert(1, (low, rounded_low[:]))
 
         out_codes = keep.tile([P, U], U32, name="out_codes", align_bytes=64)
-        out_bytes = keep.tile([P, U // 2], U8, name="out_bytes", align_bytes=64)
+        out_bytes = keep.tile([P, U], U8, name="out_bytes", align_bytes=64)
         words_out = out_1[0].rearrange("p c r -> p (c r)").bitcast(I32)
-        edges = sorted(chunk_edges | {U - LAST_PIECE})
-        store_from = {U // 2: 0, U - LAST_PIECE: U // 2, U: U - LAST_PIECE}
-        for start, stop in zip(edges, edges[1:]):
-            c, at = divmod(start, CHUNK)
-            side, side_at = divmod(start, U // 2)
+        for columns, piece in pieces:
             nc.vector.quantize_mx(
-                out_codes[:, start:stop].bitcast(FP8X4),
-                out_bytes[SCALE_ROWS * side : P, side_at : side_at + stop - start],
-                rounded[c][:, at : at + stop - start, :].rearrange("p c t -> p (c t)"),
+                out_codes[:, columns].bitcast(FP8X4), out_bytes[:, columns], piece.rearrange("p c t -> p (c t)")
             )
-            if stop in store_from:
-                ready = slice(store_from[stop], stop)
-                nc.sync.dma_start(words_out[:, ready], out_codes[:, ready].bitcast(I32))
-        scale_rows_out = out_2[0].bitcast(I32).rearrange("(q r) (side w) -> q side r w", r=SCALE_ROWS, side=2)
+        for ready in (middle, low, high):
+            nc.sync.dma_start(words_out[:, ready], out_codes[:, ready].bitcast(I32))
+        scale_rows_out = out_2[0].bitcast(I32).rearrange("(q r) w -> q r w", r=SCALE_ROWS)
         for q in range(P // QUADRANT):
             queue = nc.sync if q % 2 else nc.scalar
-            queue.dma_start(scale_rows_out[q], out_bytes[QUADRANT * q : QUADRANT * q + 2 * SCALE_ROWS, :].bitcast(I32))
+            queue.dma_start(scale_rows_out[q], out_bytes[QUADRANT * q : QUADRANT * q + SCALE_ROWS, :].bitcast(I32))

@@ -77,8 +77,8 @@ def tile_picked_snag_none_po_kernel(
         nc.sync.dma_start(xs_all[0:P:BLOCK_PARTITIONS, :].bitcast(I32), x_scales[0].bitcast(I32))
         nc.sync.dma_start(w_raw[:, ROW_PAIRS[1], :], w_rows[:, ROW_PAIRS[1], :])
         nc.sync.dma_start(ent_sb[:], ent)
-        nc.sync.dma_start(par_sb[first][:], par_rows[:, first, :])
         nc.sync.dma_start(x_all[:].bitcast(I32), x_words[0].rearrange("p c r -> p (c r)").bitcast(I32))
+        nc.sync.dma_start(par_sb[first][:], par_rows[:, first, :])
 
         nc.vector.tensor_copy(spread_bytes[:], xs_all[:].indirect(offs_sb[:]))
         for r in range(SCALE_ROWS):
@@ -113,11 +113,11 @@ def tile_picked_snag_none_po_kernel(
         nc.sync.dma_start(par_sb[last][:], par_rows[:, last, :])
         nc.sync.dma_start(vel_sb[last][:], vel_rows[:, last, :])
 
+        whole = slice(0, S)
         banks = {}
-        for t in ORDER:
+        for t in (second, first, third, last):
             cols = slice(P * t, P * (t + 1))
-            banks[t] = []
-            for entries in ENTRY_HALVES if t == first else (slice(0, S),):
+            for entries in ENTRY_HALVES if t == second else (whole,):
                 acc = psum.tile([P, entries.stop - entries.start], F32, name="acc%d_%d" % (t, entries.start))
                 nc.tensor.matmul_mx(
                     acc[:],
@@ -128,38 +128,39 @@ def tile_picked_snag_none_po_kernel(
                     start=True,
                     stop=True,
                 )
-                banks[t].append((entries, acc))
+                banks[t, entries.start] = acc
 
         def listed_by_ent(table, entries):
             return table[:].indirect(ent_sb[:, entries.start // GROUP : entries.stop // GROUP])
 
-        whole = slice(0, S)
         par_got = {t: keep.tile([P, S], F32, name="par_got%d" % t) for t in ORDER}
         vel_got = {t: keep.tile([P, S], F32, name="vel_got%d" % t) for t in ORDER[:-1]}
         vel_got[last] = placed([P, S], F32, "vel_got_last", 12 * row)
         partial = {t: keep.tile([P, S], F32, name="partial%d" % t) for t in ORDER}
         moved = {t: keep.tile([P, S], F32, name="moved%d" % t) for t in ORDER}
         grad = {
-            second: placed([P, S], F32, "grad_second", vel_at[first]),
-            third: placed([P, S], F32, "grad_third", vel_at[second]),
+            second: keep.tile([P, S], F32, name="grad_second"),
+            third: placed([P, S], F32, "grad_third", vel_at[first]),
             last: placed([P, S], F32, "grad_last", vel_at[third]),
         }
 
+        for entries in ENTRY_HALVES:
+            nc.vector.tensor_scalar_mul(grad[second][:, entries], banks[second, entries.start][:], GRAD_FACTOR)
         nc.scalar.activation(par_got[first][:], listed_by_ent(par_sb[first], whole), COPY)
-        for entries, acc in banks[first]:
+        for entries in ENTRY_HALVES:
             nc.vector.scalar_tensor_tensor(
-                partial[first][:, entries], acc[:], GRAD_FACTOR, par_got[first][:, entries], MULT, ADD
+                partial[first][:, entries], banks[first, 0][:, entries], GRAD_FACTOR, par_got[first][:, entries], MULT, ADD
             )
         for entries in ENTRY_HALVES:
             nc.scalar.activation(
                 vel_got[first][:, entries], listed_by_ent(vel_sb[first], entries), COPY, scale=VEL_FACTOR
             )
             nc.vector.tensor_tensor(moved[first][:, entries], partial[first][:, entries], vel_got[first][:, entries], ADD)
-        nc.vector.tensor_scalar_mul(grad[second][:], banks[second][0][1][:], GRAD_FACTOR)
+        nc.vector.tensor_scalar_mul(grad[third][:], banks[third, 0][:], GRAD_FACTOR)
         nc.vector.tensor_copy(listed_by_ent(par_sb[first], whole), moved[first][:])
         for t in ORDER[1:]:
-            if t != second:
-                nc.scalar.activation(grad[t][:], banks[t][0][1][:], COPY, scale=GRAD_FACTOR)
+            if t == last:
+                nc.scalar.activation(grad[t][:], banks[t, 0][:], COPY, scale=GRAD_FACTOR)
             nc.scalar.activation(par_got[t][:], listed_by_ent(par_sb[t], whole), COPY)
             nc.scalar.activation(vel_got[t][:], listed_by_ent(vel_sb[t], whole), COPY, scale=VEL_FACTOR)
             nc.gpsimd.tensor_tensor(partial[t][:], par_got[t][:], grad[t][:], ADD)
@@ -181,7 +182,7 @@ def tile_picked_snag_none_po_kernel(
 
         nc.scalar.copy(rounded_middle[:, :, first], par_sb[first][:, middle])
         nc.scalar.copy(rounded_high[:, :, first], par_sb[first][:, high])
-        gpsimd_round(staged[:, first, :], par_sb[first][:, low])
+        nc.scalar.copy(staged[:, first, :], par_sb[first][:, low])
         for t in (second, third):
             nc.scalar.copy(rounded_middle[:, :, t], par_sb[t][:, middle])
             nc.scalar.copy(staged[:, t, :], par_sb[t][:, low])
@@ -208,7 +209,7 @@ def tile_picked_snag_none_po_kernel(
             nc.vector.quantize_mx(
                 out_codes[:, columns].bitcast(FP8X4), out_bytes[:, columns], piece.rearrange("p c t -> p (c t)")
             )
-        for ready in (middle, low, high):
+        for ready, piece in pieces:
             nc.sync.dma_start(words_out[:, ready], out_codes[:, ready].bitcast(I32))
         scale_rows_out = out_2[0].bitcast(I32).rearrange("(q r) w -> q r w", r=SCALE_ROWS)
         for q in range(P // QUADRANT):

@@ -22,11 +22,9 @@ QUADRANT = 32
 SCALE_ROWS = 4
 BLOCK_PARTITIONS = 8
 GROUP = 16
-CHUNK = 256
-CHUNKS = U // CHUNK
-VECTOR_COLUMNS = CHUNK + CHUNK // 2
-GPSIMD_FROM = 2 * CHUNK + CHUNK // 2
-LAST_PIECE = CHUNK // 2
+LOW_END = 384
+HIGH_START = 640
+LAST_PIECE = 128
 ROW_PAIRS = (slice(0, 2), slice(2, 4))
 ORDER = (0, 3, 2, 1)
 VEL_FACTOR = 0.5625
@@ -130,55 +128,85 @@ def tile_picked_snag_none_po_kernel(
                 )
                 banks[t, entries.start] = acc
 
+        staged_at = 12 * row
+        par_got = {t: keep.tile([P, S], F32, name="par_got%d" % t) for t in ORDER}
+        vel_got = {t: keep.tile([P, S], F32, name="vel_got%d" % t) for t in ORDER[:-1]}
+        vel_got[last] = placed([P, S], F32, "vel_got_last", staged_at)
+        partial = {t: keep.tile([P, S], F32, name="partial%d" % t) for t in ORDER}
+        moved = {t: keep.tile([P, S], F32, name="moved%d" % t) for t in ORDER}
+        grad_second = keep.tile([P, S], F32, name="grad_second")
+        grad_third = (
+            keep.tile([P, S // 2], F32, name="grad_third_early"),
+            placed([P, S // 2], F32, "grad_third_late", vel_at[first]),
+        )
+        grad_last = placed([P, S], F32, "grad_last", vel_at[third])
+
         def listed_by_ent(table, entries):
             return table[:].indirect(ent_sb[:, entries.start // GROUP : entries.stop // GROUP])
 
-        par_got = {t: keep.tile([P, S], F32, name="par_got%d" % t) for t in ORDER}
-        vel_got = {t: keep.tile([P, S], F32, name="vel_got%d" % t) for t in ORDER[:-1]}
-        vel_got[last] = placed([P, S], F32, "vel_got_last", 12 * row)
-        partial = {t: keep.tile([P, S], F32, name="partial%d" % t) for t in ORDER}
-        moved = {t: keep.tile([P, S], F32, name="moved%d" % t) for t in ORDER}
-        grad = {
-            second: keep.tile([P, S], F32, name="grad_second"),
-            third: placed([P, S], F32, "grad_third", vel_at[first]),
-            last: placed([P, S], F32, "grad_last", vel_at[third]),
-        }
+        def gather_par(t, entries):
+            nc.scalar.activation(par_got[t][:, entries], listed_by_ent(par_sb[t], entries), COPY)
+
+        def gather_vel(t, entries):
+            nc.scalar.activation(vel_got[t][:, entries], listed_by_ent(vel_sb[t], entries), COPY, scale=VEL_FACTOR)
+
+        def add_grad(t, entries, grad):
+            nc.gpsimd.tensor_tensor(partial[t][:, entries], par_got[t][:, entries], grad, ADD)
+
+        def add_vel(engine, t, entries):
+            engine.tensor_tensor(moved[t][:, entries], partial[t][:, entries], vel_got[t][:, entries], ADD)
+
+        def scatter(t):
+            nc.vector.tensor_copy(listed_by_ent(par_sb[t], whole), moved[t][:])
 
         for entries in ENTRY_HALVES:
-            nc.vector.tensor_scalar_mul(grad[second][:, entries], banks[second, entries.start][:], GRAD_FACTOR)
-        nc.scalar.activation(par_got[first][:], listed_by_ent(par_sb[first], whole), COPY)
+            nc.vector.tensor_scalar_mul(grad_second[:, entries], banks[second, entries.start][:], GRAD_FACTOR)
+        gather_par(first, whole)
         for entries in ENTRY_HALVES:
             nc.vector.scalar_tensor_tensor(
-                partial[first][:, entries], banks[first, 0][:, entries], GRAD_FACTOR, par_got[first][:, entries], MULT, ADD
+                partial[first][:, entries],
+                banks[first, 0][:, entries],
+                GRAD_FACTOR,
+                par_got[first][:, entries],
+                MULT,
+                ADD,
             )
+        for entries, grad in zip(ENTRY_HALVES, grad_third):
+            gather_vel(first, entries)
+            add_vel(nc.vector, first, entries)
+            nc.vector.tensor_scalar_mul(grad[:], banks[third, 0][:, entries], GRAD_FACTOR)
+        scatter(first)
+
         for entries in ENTRY_HALVES:
-            nc.scalar.activation(
-                vel_got[first][:, entries], listed_by_ent(vel_sb[first], entries), COPY, scale=VEL_FACTOR
-            )
-            nc.vector.tensor_tensor(moved[first][:, entries], partial[first][:, entries], vel_got[first][:, entries], ADD)
-        nc.vector.tensor_scalar_mul(grad[third][:], banks[third, 0][:], GRAD_FACTOR)
-        nc.vector.tensor_copy(listed_by_ent(par_sb[first], whole), moved[first][:])
-        for t in ORDER[1:]:
-            if t == last:
-                nc.scalar.activation(grad[t][:], banks[t, 0][:], COPY, scale=GRAD_FACTOR)
-            nc.scalar.activation(par_got[t][:], listed_by_ent(par_sb[t], whole), COPY)
-            nc.scalar.activation(vel_got[t][:], listed_by_ent(vel_sb[t], whole), COPY, scale=VEL_FACTOR)
-            nc.gpsimd.tensor_tensor(partial[t][:], par_got[t][:], grad[t][:], ADD)
-            nc.gpsimd.tensor_tensor(moved[t][:], partial[t][:], vel_got[t][:], ADD)
-            nc.vector.tensor_copy(listed_by_ent(par_sb[t], whole), moved[t][:])
+            gather_par(second, entries)
+            add_grad(second, entries, grad_second[:, entries])
+        for entries in ENTRY_HALVES:
+            gather_vel(second, entries)
+            add_vel(nc.gpsimd, second, entries)
+        scatter(second)
+
+        gather_par(third, whole)
+        for entries, grad in zip(ENTRY_HALVES, grad_third):
+            add_grad(third, entries, grad[:])
+        gather_vel(third, whole)
+        add_vel(nc.gpsimd, third, whole)
+        scatter(third)
+
+        nc.scalar.activation(grad_last[:], banks[last, 0][:], COPY, scale=GRAD_FACTOR)
+        gather_par(last, whole)
+        add_grad(last, whole, grad_last[:])
+        gather_vel(last, whole)
+        add_vel(nc.gpsimd, last, whole)
+        scatter(last)
         for t in ORDER:
             nc.sync.dma_start(out_rows[:, t, :], par_sb[t][:])
 
-        edges = (0, VECTOR_COLUMNS, GPSIMD_FROM, U)
-        low, middle, high = (slice(start, stop) for start, stop in zip(edges, edges[1:]))
-        staged = placed([P, PACK, VECTOR_COLUMNS], BF16, "staged", 12 * row)
-        rounded_low = keep.tile([P, VECTOR_COLUMNS, PACK], BF16, name="rounded_low", align_bytes=64)
-        middle_bytes = 2 * PACK * (middle.stop - middle.start)
-        rounded_middle = placed([P, middle.stop - middle.start, PACK], BF16, "rounded_middle", vel_at[last])
-        rounded_high = placed([P, high.stop - high.start, PACK], BF16, "rounded_high", vel_at[last] + middle_bytes)
-
-        def gpsimd_round(out, in_):
-            nc.gpsimd.tensor_scalar(out, in_, 1.0, -0.0, MULT, ADD)
+        low, middle, high = slice(0, LOW_END), slice(LOW_END, HIGH_START), slice(HIGH_START, U)
+        staged = placed([P, PACK, LOW_END], BF16, "staged", staged_at)
+        rounded_low = keep.tile([P, LOW_END, PACK], BF16, name="rounded_low", align_bytes=64)
+        middle_bytes = 2 * PACK * (HIGH_START - LOW_END)
+        rounded_middle = placed([P, HIGH_START - LOW_END, PACK], BF16, "rounded_middle", vel_at[last])
+        rounded_high = placed([P, U - HIGH_START, PACK], BF16, "rounded_high", vel_at[last] + middle_bytes)
 
         nc.scalar.copy(rounded_middle[:, :, first], par_sb[first][:, middle])
         nc.scalar.copy(rounded_high[:, :, first], par_sb[first][:, high])
@@ -186,13 +214,17 @@ def tile_picked_snag_none_po_kernel(
         for t in (second, third):
             nc.scalar.copy(rounded_middle[:, :, t], par_sb[t][:, middle])
             nc.scalar.copy(staged[:, t, :], par_sb[t][:, low])
-            gpsimd_round(rounded_high[:, :, t], par_sb[t][:, high])
-        pieces = [(middle, rounded_middle[:])]
-        for at, stop in ((0, CHUNK), (CHUNK, CHUNK + LAST_PIECE)):
-            pieces.append((slice(high.start + at, high.start + stop), rounded_high[:, at:stop, :]))
-        for columns, piece in pieces:
-            nc.scalar.copy(piece[:, :, last], par_sb[last][:, columns])
-        low_halves = (slice(0, VECTOR_COLUMNS // 2), slice(VECTOR_COLUMNS // 2, VECTOR_COLUMNS))
+            nc.gpsimd.tensor_scalar(rounded_high[:, :, t], par_sb[t][:, high], 1.0, -0.0, MULT, ADD)
+
+        last_start = U - LAST_PIECE
+        middle_piece = (middle, rounded_middle[:])
+        high_pieces = [
+            (slice(HIGH_START, last_start), rounded_high[:, : last_start - HIGH_START, :]),
+            (slice(last_start, U), rounded_high[:, last_start - HIGH_START :, :]),
+        ]
+        for columns, rounded in [middle_piece] + high_pieces:
+            nc.scalar.copy(rounded[:, :, last], par_sb[last][:, columns])
+        low_halves = (slice(0, LOW_END // 2), slice(LOW_END // 2, LOW_END))
         for half in low_halves:
             nc.vector.tensor_copy(staged[:, last, half], par_sb[last][:, half])
         for half in low_halves:
@@ -200,17 +232,17 @@ def tile_picked_snag_none_po_kernel(
                 rounded_low[:, half, :].rearrange("p (a i) t -> p a t i", i=PACK),
                 staged[:, :, half].rearrange("p t (a i) -> p a t i", i=PACK),
             )
-        pieces.insert(1, (low, rounded_low[:]))
 
+        pieces = [middle_piece, (low, rounded_low[:])] + high_pieces
         out_codes = keep.tile([P, U], U32, name="out_codes", align_bytes=64)
         out_bytes = keep.tile([P, U], U8, name="out_bytes", align_bytes=64)
         words_out = out_1[0].rearrange("p c r -> p (c r)").bitcast(I32)
-        for columns, piece in pieces:
+        for columns, rounded in pieces:
             nc.vector.quantize_mx(
-                out_codes[:, columns].bitcast(FP8X4), out_bytes[:, columns], piece.rearrange("p c t -> p (c t)")
+                out_codes[:, columns].bitcast(FP8X4), out_bytes[:, columns], rounded.rearrange("p c t -> p (c t)")
             )
-        for ready, piece in pieces:
-            nc.sync.dma_start(words_out[:, ready], out_codes[:, ready].bitcast(I32))
+        for columns in (middle, low, high):
+            nc.sync.dma_start(words_out[:, columns], out_codes[:, columns].bitcast(I32))
         scale_rows_out = out_2[0].bitcast(I32).rearrange("(q r) w -> q r w", r=SCALE_ROWS)
         for q in range(P // QUADRANT):
             queue = nc.sync if q % 2 else nc.scalar

from contextlib import ExitStack

import concourse.mybir as mybir

K, T, S, N, U = 512, 2048, 512, 512, 1024
FLOPS = 2 * K * N * S

F32 = mybir.dt.float32
BF16 = mybir.dt.bfloat16
I32 = mybir.dt.int32
U32 = mybir.dt.uint32
U16 = mybir.dt.uint16
U8 = mybir.dt.uint8
FP8X4 = mybir.dt.float8_e4m3fn_x4
MULT = mybir.AluOpType.mult
ADD = mybir.AluOpType.add
COPY = mybir.ActivationFunctionType.Copy

P = 128
PACK = 4
QUADRANT = 32
SCALE_ROWS = 4
BLOCK_PARTITIONS = 8
GROUP = 16
LOW_END = 384
HIGH_START = 640
LAST_PIECE = 128
ROW_PAIRS = (slice(0, 2), slice(2, 4))
ORDER = (0, 3, 2, 1)
VEL_FACTOR = 0.5625
GRAD_FACTOR = -0.4375
ENTRY_HALVES = (slice(0, S // 2), slice(S // 2, S))


def tile_picked_snag_none_po_kernel(
    tc, x_words, x_scales, w1, par, vel, offs, ent, out_0, out_1, out_2
):
    nc = tc.nc
    par_rows = par.rearrange("(p t) c -> p t c", t=PACK)
    vel_rows = vel.rearrange("(p t) c -> p t c", t=PACK)
    out_rows = out_0.rearrange("(p t) c -> p t c", t=PACK)
    first, second, third, last = ORDER

    with ExitStack() as ctx:
        keep = ctx.enter_context(tc.tile_pool(name="keep", bufs=1))
        shared = ctx.enter_context(tc.tile_pool(name="shared", bufs=1))
        psum = ctx.enter_context(tc.psum_pool(name="psum", bufs=1))

        offs_sb = keep.tile([P, S // GROUP], U16, name="offs_sb")
        ent_sb = keep.tile([P, S // GROUP], U16, name="ent_sb")

        def placed(shape, dtype, name, offset):
            return shared.tile(shape, dtype, name=name, offset=offset, align_bytes=64)

        row = 4 * U
        lap = 64
        w_raw = placed([P, PACK, N], F32, "w_raw", row)
        x_all = placed([P, T], U32, "x_all", 6 * row)
        xs_all = placed([P, T], U8, "xs_all", 11 * row)
        par_at = {second: lap, third: 2 * row + lap, last: 6 * row + lap}
        vel_at = {first: 10 * row + lap, second: row + lap, third: 5 * row + lap, last: 8 * row - lap}
        par_sb = {t: placed([P, U], F32, "par%d" % t, par_at[t]) for t in ORDER[1:]}
        par_sb[first] = keep.tile([P, U], F32, name="par_first")
        vel_sb = {t: placed([P, U], F32, "vel%d" % t, vel_at[t]) for t in ORDER}
        x_codes = keep.tile([P, S], U32, name="x_codes", align_bytes=64)
        x_bytes = keep.tile([P, S], U8, name="x_bytes", align_bytes=64)
        spread_bytes = keep.tile([P, S], U8, name="spread_bytes", align_bytes=64)

        nc.vector.memset(xs_all[:].bitcast(I32), 0)
        nc.gpsimd.memset(x_bytes[:].bitcast(I32), 0)

        w_rows = w1.rearrange("(p j) c -> p j c", j=PACK)
        nc.sync.dma_start(w_raw[:, ROW_PAIRS[0], :], w_rows[:, ROW_PAIRS[0], :])
        nc.sync.dma_start(offs_sb[:], offs)
        nc.sync.dma_start(xs_all[0:P:BLOCK_PARTITIONS, :].bitcast(I32), x_scales[0].bitcast(I32))
        nc.sync.dma_start(w_raw[:, ROW_PAIRS[1], :], w_rows[:, ROW_PAIRS[1], :])
        nc.sync.dma_start(ent_sb[:], ent)
        nc.sync.dma_start(x_all[:].bitcast(I32), x_words[0].rearrange("p c r -> p (c r)").bitcast(I32))
        nc.sync.dma_start(par_sb[first][:], par_rows[:, first, :])

        nc.vector.tensor_copy(spread_bytes[:], xs_all[:].indirect(offs_sb[:]))
        for r in range(SCALE_ROWS):
            nc.sync.dma_start(
                x_bytes[r:P:QUADRANT, :].bitcast(I32),
                spread_bytes[BLOCK_PARTITIONS * r : P : QUADRANT, :].bitcast(I32),
            )
        nc.sync.dma_start(vel_sb[first][:], vel_rows[:, first, :])

        w_codes = keep.tile([P, N], U32, name="w_codes", align_bytes=64)
        w_bytes = keep.tile([P, N], U8, name="w_bytes", align_bytes=64)
        w_view = w_raw[:].rearrange("p j (a m t) -> p a t m j", m=2, t=PACK)
        w_dealt = []
        for h, second_pair_copy in enumerate((nc.vector.tensor_copy, nc.scalar.copy)):
            dealt = keep.tile([P, N * 2], BF16, name="w_dealt%d" % h, align_bytes=64)
            dealt_view = dealt[:].rearrange("p (t a m j) -> p a t m j", t=2, m=2, j=PACK)
            for pair_copy, pair in zip((nc.scalar.copy, second_pair_copy), ROW_PAIRS):
                pair_copy(dealt_view[:, :, :, :, pair], w_view[:, :, 2 * h : 2 * h + 2, :, pair])
            w_dealt.append(dealt)
        nc.sync.dma_start(par_sb[second][:], par_rows[:, second, :])
        nc.sync.dma_start(vel_sb[second][:], vel_rows[:, second, :])
        nc.sync.dma_start(par_sb[third][:], par_rows[:, third, :])

        for h in range(2):
            cols = slice(2 * P * h, 2 * P * (h + 1))
            nc.vector.quantize_mx(w_codes[:, cols].bitcast(FP8X4), w_bytes[:, cols], w_dealt[h][:])

        for entries in ENTRY_HALVES:
            listed = offs_sb[:, entries.start // GROUP : entries.stop // GROUP]
            nc.vector.tensor_copy(x_codes[:, entries], x_all[:].indirect(listed))
        nc.sync.dma_start(vel_sb[third][:], vel_rows[:, third, :])
        nc.sync.dma_start(par_sb[last][:], par_rows[:, last, :])
        nc.sync.dma_start(vel_sb[last][:], vel_rows[:, last, :])

        whole = slice(0, S)
        banks = {}
        for t in (second, first, third, last):
            cols = slice(P * t, P * (t + 1))
            for entries in ENTRY_HALVES if t == second else (whole,):
                acc = psum.tile([P, entries.stop - entries.start], F32, name="acc%d_%d" % (t, entries.start))
                nc.tensor.matmul_mx(
                    acc[:],
                    lhsT=w_codes[:, cols].bitcast(FP8X4),
                    lhsT_scale=w_bytes[:, cols],
                    rhs=x_codes[:, entries].bitcast(FP8X4),
                    rhs_scale=x_bytes[:, entries],
                    start=True,
                    stop=True,
                )
                banks[t, entries.start] = acc

        staged_at = 12 * row
        par_got = {t: keep.tile([P, S], F32, name="par_got%d" % t) for t in ORDER}
        vel_got = {t: keep.tile([P, S], F32, name="vel_got%d" % t) for t in ORDER[:-1]}
        vel_got[last] = placed([P, S], F32, "vel_got_last", staged_at)
        partial = {t: keep.tile([P, S], F32, name="partial%d" % t) for t in ORDER}
        moved = {t: keep.tile([P, S], F32, name="moved%d" % t) for t in ORDER}
        grad_second = keep.tile([P, S], F32, name="grad_second")
        grad_third = (
            keep.tile([P, S // 2], F32, name="grad_third_early"),
            placed([P, S // 2], F32, "grad_third_late", vel_at[first]),
        )
        grad_last = placed([P, S], F32, "grad_last", vel_at[third])

        def listed_by_ent(table, entries):
            return table[:].indirect(ent_sb[:, entries.start // GROUP : entries.stop // GROUP])

        def gather_par(t, entries):
            nc.scalar.activation(par_got[t][:, entries], listed_by_ent(par_sb[t], entries), COPY)

        def gather_vel(t, entries):
            nc.scalar.activation(vel_got[t][:, entries], listed_by_ent(vel_sb[t], entries), COPY, scale=VEL_FACTOR)

        def add_grad(t, entries, grad):
            nc.gpsimd.tensor_tensor(partial[t][:, entries], par_got[t][:, entries], grad, ADD)

        def add_vel(engine, t, entries):
            engine.tensor_tensor(moved[t][:, entries], partial[t][:, entries], vel_got[t][:, entries], ADD)

        def scatter(t):
            nc.vector.tensor_copy(listed_by_ent(par_sb[t], whole), moved[t][:])

        for entries in ENTRY_HALVES:
            nc.vector.tensor_scalar_mul(grad_second[:, entries], banks[second, entries.start][:], GRAD_FACTOR)
        gather_par(first, whole)
        for entries in ENTRY_HALVES:
            nc.vector.scalar_tensor_tensor(
                partial[first][:, entries],
                banks[first, 0][:, entries],
                GRAD_FACTOR,
                par_got[first][:, entries],
                MULT,
                ADD,
            )
        for entries, grad in zip(ENTRY_HALVES, grad_third):
            gather_vel(first, entries)
            add_vel(nc.vector, first, entries)
            nc.vector.tensor_scalar_mul(grad[:], banks[third, 0][:, entries], GRAD_FACTOR)
        scatter(first)

        for entries in ENTRY_HALVES:
            gather_par(second, entries)
            add_grad(second, entries, grad_second[:, entries])
        for entries in ENTRY_HALVES:
            gather_vel(second, entries)
            add_vel(nc.gpsimd, second, entries)
        scatter(second)

        gather_par(third, whole)
        for entries, grad in zip(ENTRY_HALVES, grad_third):
            add_grad(third, entries, grad[:])
        gather_vel(third, whole)
        add_vel(nc.gpsimd, third, whole)
        scatter(third)

        nc.scalar.activation(grad_last[:], banks[last, 0][:], COPY, scale=GRAD_FACTOR)
        gather_par(last, whole)
        add_grad(last, whole, grad_last[:])
        gather_vel(last, whole)
        add_vel(nc.gpsimd, last, whole)
        scatter(last)
        for t in ORDER:
            nc.sync.dma_start(out_rows[:, t, :], par_sb[t][:])

        low, middle, high = slice(0, LOW_END), slice(LOW_END, HIGH_START), slice(HIGH_START, U)
        staged = placed([P, PACK, LOW_END], BF16, "staged", staged_at)
        rounded_low = keep.tile([P, LOW_END, PACK], BF16, name="rounded_low", align_bytes=64)
        middle_bytes = 2 * PACK * (HIGH_START - LOW_END)
        rounded_middle = placed([P, HIGH_START - LOW_END, PACK], BF16, "rounded_middle", vel_at[last])
        rounded_high = placed([P, U - HIGH_START, PACK], BF16, "rounded_high", vel_at[last] + middle_bytes)

        nc.scalar.copy(rounded_middle[:, :, first], par_sb[first][:, middle])
        nc.scalar.copy(rounded_high[:, :, first], par_sb[first][:, high])
        nc.scalar.copy(staged[:, first, :], par_sb[first][:, low])
        for t in (second, third):
            nc.scalar.copy(rounded_middle[:, :, t], par_sb[t][:, middle])
            nc.scalar.copy(staged[:, t, :], par_sb[t][:, low])
            nc.gpsimd.tensor_scalar(rounded_high[:, :, t], par_sb[t][:, high], 1.0, -0.0, MULT, ADD)

        last_start = U - LAST_PIECE
        middle_piece = (middle, rounded_middle[:])
        high_pieces = [
            (slice(HIGH_START, last_start), rounded_high[:, : last_start - HIGH_START, :]),
            (slice(last_start, U), rounded_high[:, last_start - HIGH_START :, :]),
        ]
        for columns, rounded in [middle_piece] + high_pieces:
            nc.scalar.copy(rounded[:, :, last], par_sb[last][:, columns])
        low_halves = (slice(0, LOW_END // 2), slice(LOW_END // 2, LOW_END))
        for half in low_halves:
            nc.vector.tensor_copy(staged[:, last, half], par_sb[last][:, half])
        for half in low_halves:
            nc.vector.tensor_copy(
                rounded_low[:, half, :].rearrange("p (a i) t -> p a t i", i=PACK),
                staged[:, :, half].rearrange("p t (a i) -> p a t i", i=PACK),
            )

        pieces = [middle_piece, (low, rounded_low[:])] + high_pieces
        out_codes = keep.tile([P, U], U32, name="out_codes", align_bytes=64)
        out_bytes = keep.tile([P, U], U8, name="out_bytes", align_bytes=64)
        words_out = out_1[0].rearrange("p c r -> p (c r)").bitcast(I32)
        for columns, rounded in pieces:
            nc.vector.quantize_mx(
                out_codes[:, columns].bitcast(FP8X4), out_bytes[:, columns], rounded.rearrange("p c t -> p (c t)")
            )
        for columns in (middle, low, high):
            nc.sync.dma_start(words_out[:, columns], out_codes[:, columns].bitcast(I32))
        scale_rows_out = out_2[0].bitcast(I32).rearrange("(q r) w -> q r w", r=SCALE_ROWS)
        for q in range(P // QUADRANT):
            queue = nc.sync if q % 2 else nc.scalar
            queue.dma_start(scale_rows_out[q], out_bytes[QUADRANT * q : QUADRANT * q + SCALE_ROWS, :].bitcast(I32))
